import numpy as np
CORES = [45,53,77,117,47,55,79,119]
N = 8
T, FF, CAP, CAPP = 4096, 2, 1024, 256
def entries(a): return a.T.reshape(-1)
def pack(v, P): return np.ascontiguousarray(np.asarray(v, np.int32).reshape(-1, P).T)
def lists(rng, how):
    O = np.stack([rng.permutation(np.repeat(np.arange(N), CAPP))[:CAP] for k in range(N)])
    if how == "apart": s = int(rng.integers(N * CAPP - CAP + 1)); cnt = np.bincount(np.repeat(np.arange(N), CAPP)[s:s + CAP], minlength=N); a = rng.permutation(N); O = np.stack([rng.permutation(np.repeat(np.arange(N), cnt[(a + k) % N])) for k in rng.permutation(N)])
    if how == "full": z = rng.permutation(N); O = np.stack([rng.permutation(np.repeat(z, CAPP)[:CAP]) for k in range(N)])
    if how == "none": z = int(rng.integers(N)); O = np.stack([rng.permutation(np.repeat(np.delete(np.arange(N), z), CAPP))[:CAP] for k in range(N)])
    P = np.zeros((N, CAP), np.int64)
    for o in range(N):
        q = rng.permutation(T); u = 0
        for k in range(N):
            m = np.nonzero(O[k] == o)[0]
            if how != "apart": q = rng.permutation(T); u = 0
            if how == "sorted": q = np.r_[0, T - 1, 1 + rng.permutation(T - 2)]
            P[k, m] = T * o + q[u:u + len(m)]; u += len(m)
    if how == "same": P = np.stack([rng.permutation(P[0]) for k in range(N)])
    if how == "sorted": P = np.sort(P, axis=1)
    G = 2 * rng.random((N, 16, CAP // 16), dtype=np.float32) - 1
    if how == "none": G[rng.random(G.shape) < 0.125] = 0
    return {"gate": G, "pick": np.stack([pack(p, 16) for p in P])}
def setup_inputs(rng):
    return dict({"x": rng.standard_normal((N, 128, T), dtype=np.float32), "w1": (rng.standard_normal((N, 128, FF * 128), dtype=np.float32) / 8), "w2": (rng.standard_normal((N, 128, FF * 128), dtype=np.float32) / 16)}, **lists(rng, "uniform"))
def setup_inputs_apart(rng):
    d = setup_inputs(rng); d.update(lists(rng, "apart"))
    for k in ("x",): d[k] = (d[k].astype(np.float32) * 1024.0).astype(d[k].dtype)
    return d
def setup_inputs_full(rng):
    d = setup_inputs(rng); d.update(lists(rng, "full"))
    for k in ("x",): d[k] = (d[k].astype(np.float32) * (1 / 1024.0)).astype(d[k].dtype)
    return d
def setup_inputs_none(rng):
    d = setup_inputs(rng); d.update(lists(rng, "none"))
    return d
def setup_inputs_same(rng):
    d = setup_inputs(rng); d.update(lists(rng, "same"))
    return d
def setup_inputs_sorted(rng):
    d = setup_inputs(rng); d.update(lists(rng, "sorted"))
    return d
def check_inputs(x):
    bad = []
    if x["pick"].min() < 0 or x["pick"].max() >= N * T: bad.append("pick out of range")
    if any(len(np.unique(a)) != a.size for a in x["pick"]): bad.append("a token stands twice in a list")
    if max(int(np.bincount(entries(a) // T, minlength=N).max()) for a in x["pick"]) > CAPP: bad.append("more than CAPP of an expert's tokens lie on one rank")
    return bad
def reference(x, w1, w2, gate, pick):
    X, W1, W2 = x.astype(np.float64), w1.astype(np.float64), w2.astype(np.float64)
    A = np.concatenate(list(X), axis=1); Y = np.zeros((128, N * T))
    for k in range(N):
        P = entries(pick[k]); g = entries(gate[k]).astype(np.float64)
        Y[:, P] += g[None, :] * sum(W2[k][:, 128 * f:128 * f + 128].T @ np.maximum(W1[k][:, 128 * f:128 * f + 128].T @ A[:, P], 0.0) for f in range(FF))
    return {"y": np.stack([Y[:, T * r:T * r + T] for r in range(N)]).astype(np.float32)}

@@ -1,0 +1,374 @@
+from concourse.bass import DstId, RemoteDMATransfer
+from concourse.mybir import AluOpType as A, ActivationFunctionType as F
+
+N, NT, CP = 8, 4096, 256
+NX = NT + CP
+ZC = NX // 4
+
+SCRATCH = {
+    "pk": ("sbuf", [128, 8], "int32"), "rk": ("sbuf", [128, 8], "int32"), "tk": ("sbuf", [128, 8], "int32"),
+    "t1": ("sbuf", [128, 8], "int32"), "ds": ("sbuf", [128, 8], "float32"), "dd": ("sbuf", [128, 8], "float32"),
+    "ror": ("sbuf", [128, 64], "bfloat16"), "rp": ("sbuf", [128, 64], "float32"), "scn": ("sbuf", [128, 64], "float32"),
+    "a32": ("sbuf", [128, 8], "int32"), "v32": ("sbuf", [128, 8], "int32"), "ibits": ("sbuf", [128, 32], "int32"),
+    "ff": ("sbuf", [128, 40], "float32"),
+    "nb": ("sbuf", [128, 1024], "bfloat16"), "oh": ("sbuf", [128, 1024], "bfloat16"), "ol": ("sbuf", [128, 1024], "bfloat16"),
+    "tabs": ("sbuf", [128, 1024], "uint16"),
+    "ones": ("sbuf", [128, 128], "bfloat16"), "tri": ("sbuf", [128, 128], "bfloat16"),
+    "iob": ("sbuf", [128, 128], "bfloat16"), "ion": ("sbuf", [128, 128], "bfloat16"),
+    "padc": ("sbuf", [128, 128], "bfloat16"), "c4k": ("sbuf", [128, 128], "bfloat16"), "u256": ("sbuf", [128, 64], "bfloat16"),
+    "upat": ("sbuf", [128, 64], "float32"), "seg": ("sbuf", [128, 64], "float32"),
+    "onesf": ("sbuf", [128, 512], "float32"), "diag": ("sbuf", [128, 512], "float32"),
+    "iobf": ("sbuf", [128, 128], "float32"), "iorc": ("sbuf", [128, 32], "float32"),
+    "expi": ("sbuf", [128, 32], "int32"), "expu": ("sbuf", [128, 32], "uint16"),
+    "spay": ("sbuf", [128, 24], "float32"),
+    "gob": ("sbuf", [128, 2048], "float32"), "gor": ("sbuf", [128, 512], "float32"),
+    "gws": ("sbuf", [128, 64], "float32"), "gx": ("sbuf", [128, 512], "float32"), "gbs": ("sbuf", [128, 512], "float32"),
+    "wo": ("sbuf", [128, 512], "float32"), "sw": ("sbuf", [128, 512], "float32"), "rlw": ("sbuf", [128, 512], "float32"),
+    "rlp": ("sbuf", [128, 24], "float32"), "rlt": ("sbuf", [128, 128], "uint16"),
+    "xs": ("sbuf", [128, NX], "float32"), "ys": ("sbuf", [128, NX], "float32"),
+    "vt": ("sbuf", [128, 2048], "float32"), "tv": ("sbuf", [128, 512], "float32"),
+    "hs": ("sbuf", [128, 1024], "float32"), "rs": ("sbuf", [128, 2048], "float32"), "tmp": ("sbuf", [128, 256], "float32"),
+}
+for _i in range(8):
+    SCRATCH["b%d" % _i] = ("psum", [128, 512], "float32")
+SEMAPHORES = (["cg", "cv", "cs", "ct", "loc", "wsent", "dpick", "dgate", "dw0", "dw1", "dx", "dy", "pay", "w0", "w1",
+               "rw0", "rw1", "rpay", "rtab", "tok0", "tok1"]
+              + ["tab%d" % k for k in range(N)] + ["res%d" % k for k in range(N)])
+
+
+def layout(T, topo):
+    cores = list(T.cores)
+    every = range(topo.CHIPS * topo.CORES_PER_CHIP)
+    chips = []
+    for c in cores:
+        if topo.chip(c) not in chips:
+            chips.append(topo.chip(c))
+
+    def free(c):
+        return all(topo.may_write(c, d) for d in cores if d != c)
+
+    members = {ch: [k for k in range(N) if topo.chip(cores[k]) == ch] for ch in chips}
+    helpers = {ch: [c for c in every if topo.chip(c) == ch and c not in cores] for ch in chips}
+    relays, trelay = {}, {}
+    for k in range(N):
+        ports = [h for h in helpers[topo.chip(cores[k])] if free(h)]
+        near = [h for h in ports if topo.die(h) == topo.die(cores[k])]
+        far = [h for h in ports if topo.die(h) != topo.die(cores[k])]
+        use = (near or far) if free(cores[k]) else (far or near)
+        relays[k] = [use[0], use[-1]]
+        trelay[k] = None if free(cores[k]) else (near or far)[0]
+    server, serves = {}, {}
+    for ch in chips:
+        left = list(helpers[ch])
+        foreign = [k for k in range(N) if k not in members[ch]]
+        for k in sorted(foreign, key=lambda q: (not free(cores[q]), q)):
+            die = topo.die(relays[k][0])
+            h = ([c for c in left if topo.die(c) == die] or left)[0]
+            left.remove(h)
+            server[ch, k] = h
+            serves[h] = k
+    far_servers = {k: [server[ch, k] for ch in chips if ch != topo.chip(cores[k])] for k in range(N)}
+    partner = {k: [q for q in members[topo.chip(cores[k])] if q != k][0] for k in range(N)}
+    pay = {k: [cores[partner[k]]] + far_servers[k] for k in range(N)}
+    tab = {k: [cores[q] for q in range(N) if q != k] for k in range(N)}
+    order = {}
+    for ch in chips:
+        for i, h in enumerate(helpers[ch]):
+            m = members[ch]
+            order[h] = m if i % 2 == 0 else m[::-1]
+    return {"cores": cores, "chips": chips, "members": members, "helpers": helpers, "relays": relays, "trelay": trelay,
+            "server": server, "serves": serves, "far_servers": far_servers, "partner": partner, "pay": pay, "tab": tab,
+            "order": order}
+
+
+def rank_program(g, core, T, topo):
+    L = layout(T, topo)
+    cores = L["cores"]
+    ch = topo.chip(core)
+    if ch not in L["chips"]:
+        return
+    rank = T.rank_of(core)
+    Q = {"g": g, "v": g.vector, "s": g.scalar, "t": g.tensor, "d": g.sync}
+    V, S, P = g.vector, g.scalar, g.tensor
+    count, seen = {"loc": 0}, {}
+
+    def wait(q, *deps):
+        for sem, val in deps:
+            if seen.get((q, sem), 0) < val:
+                Q[q].wait_ge(T.sem[sem], val)
+                seen[q, sem] = val
+
+    def done(q, ins):
+        name = "c" + q
+        count[name] = count.get(name, 0) + 1
+        ins.then_inc(T.sem[name], 1)
+        return (name, count[name])
+
+    def engines(src, dsts):
+        m = topo.mask(src, dsts[0])
+        for d in dsts[1:]:
+            m &= topo.mask(src, d)
+        return m
+
+    def ways(src, dsts):
+        return bin(engines(src, dsts)).count("1")
+
+    def send(targets, src_ap, rsem):
+        m = engines(core, [c for c, ap in targets])
+        if len(targets) == 1:
+            rid, pid, se = topo.addr(targets[0][0])
+            g.remote_dma(out_ap=targets[0][1], in_ap=src_ap, remote_sem=T.sem[rsem], local_sem=T.sem.loc, pid=pid,
+                         routing_id=rid, dma_engine_mask=m)
+        else:
+            ids = []
+            for c, ap in targets:
+                rid, pid, se = topo.addr(c)
+                ids.append(DstId(rid=rid, pnc=pid))
+            g.remote_dma_fused([RemoteDMATransfer(dst_ids=ids, dma_engine_mask=m, remote_sem=T.sem[rsem], srcs=[src_ap],
+                                                  dsts=[ap for c, ap in targets])], local_sem=T.sem.loc)
+        count["loc"] += bin(m).count("1")
+
+    def split(k, dsts):
+        direct = [d for d in dsts if topo.may_write(cores[k], d)]
+        return direct, [d for d in dsts if d not in direct]
+
+    def arrival(k, dsts, me):
+        direct, rest = split(k, dsts)
+        return ways(cores[k], direct) if me in direct else ways(L["trelay"][k], rest)
+
+    def gate_consts(rl):
+        n = 16 * len(rl)
+        d1 = done("v", V.memset(T.onesf[:, 0:512], 1.0))
+        done("g", g.iota(T.iobf[:, :], [[0, 8], [1, 16]], 0, 0, allow_small_or_imprecise_dtypes=True))
+        step = 16 * (rl[-1] - rl[0])
+        done("g", g.iota(T.iorc[:, 0:n], [[step, len(rl)], [1, 16]], 16 * rl[0], 0, allow_small_or_imprecise_dtypes=True))
+        done("g", g.iota(T.expi[:, :], [[1, 32]], 0, 0))
+        wait("g", d1)
+        return done("g", g.affine_select(T.diag[:, 0:16 * n], T.onesf[:, 0:16 * n], [[0, n], [1, 16]], A.is_equal, 0.0, 0, -1))
+
+    def gate_columns(ready, pay, pdeps, n, i, gw, gb, free_gw, free_gb):
+        wait("v", ready, *pdeps)
+        ob, orc, dl = 1024 * i, 256 * i, []
+        for m in range(8):
+            done("v", V.tensor_scalar(T.gob[:, ob + 128 * m:ob + 128 * m + 128], T.iobf[:, :], pay[:, 8 + m:9 + m], None, A.is_equal))
+            dl.append(done("v", V.tensor_scalar(T.gor[:, orc + n * m:orc + n * m + n], T.iorc[:, 0:n], pay[:, 16 + m:17 + m],
+                                                pay[:, m:m + 1], A.is_equal, A.mult)))
+        wait("t", *free_gw)
+        for m in range(8):
+            wait("t", dl[m])
+            ins = P.matmul(out=gw[:, 0:n], lhsT=T.gob[:, ob + 128 * m:ob + 128 * m + 128], rhs=T.gor[:, orc + n * m:orc + n * m + n],
+                           start=m == 0, stop=m == 7)
+        d = done("t", ins)
+        wait("v", d)
+        d = done("v", V.tensor_copy(T.gws[:, 32 * i:32 * i + n], gw[:, 0:n]))
+        wait("v", d)
+        c = 256 * i
+        d = done("v", V.tensor_tensor(T.gx[:, c:c + 16 * n], T.gws[:, 32 * i:32 * i + n].indirect(T.expu[:, 0:n]),
+                                      T.diag[:, 0:16 * n], A.mult))
+        wait("t", d, *free_gb)
+        d = done("t", P.matmul(out=gb[:, 0:16 * n], lhsT=T.onesf[0:16, 0:128], rhs=T.gx[0:16, c:c + 16 * n], start=True, stop=True))
+        wait("s", d)
+        return done("s", S.activation(T.gbs[:, c:c + 16 * n], gb[:, 0:16 * n], F.Copy))
+
+    def expert(w, wdeps, rhs, rdeps, h0, h1, ob, i):
+        wait("t", wdeps[0], *rdeps)
+        hp, c, e = [h0, h1], [], []
+        for f in range(2):
+            c.append(done("t", P.matmul(out=hp[f][:, 0:256], lhsT=w[:, 128 * f:128 * f + 128], rhs=rhs, start=True, stop=True)))
+        for f in range(2):
+            a = 512 * i + 256 * f
+            wait("s", c[f])
+            e.append(done("s", S.activation(T.hs[:, a:a + 256], hp[f][:, 0:256], F.Relu)))
+        wait("t", wdeps[1])
+        for f in range(2):
+            a = 512 * i + 256 * f
+            wait("t", e[f])
+            ins = P.matmul(out=ob[:, 0:256], lhsT=w[:, 256 + 128 * f:384 + 128 * f], rhs=T.hs[:, a:a + 256], start=f == 0, stop=f == 1)
+        return done("t", ins)
+
+    def finish():
+        for name in ("cg", "cv", "cs", "ct", "loc"):
+            if count.get(name, 0):
+                wait("g", (name, count[name]))
+
+    if rank is None:
+        k = L["serves"][core]
+        rl = sorted(L["members"][ch])
+        ready = gate_consts(rl)
+        wait("v", ready)
+        ready = done("v", V.tensor_copy(T.expu[:, :], T.expi[:, :]))
+        for f in range(2):
+            for q in L["members"][ch]:
+                if L["relays"][q][f] == core:
+                    wait("g", ("rw%d" % f, ways(cores[q], [core])))
+                    send([(h, T.sw[:, 256 * f:256 * f + 256]) for h in L["far_servers"][q]], T.rlw[:, 256 * f:256 * f + 256], "w%d" % f)
+        for q in L["members"][ch]:
+            if L["trelay"][q] == core:
+                wait("g", ("rpay", ways(cores[q], [core])))
+                send([(h, T.spay[:, :]) for h in split(q, L["pay"][q])[1]], T.rlp[:, :], "pay")
+                wait("g", ("rtab", ways(cores[q], [core])))
+                send([(c, T.tabs[:, 128 * q:128 * q + 128]) for c in split(q, L["tab"][q])[1]], T.rlt[:, :], "tab%d" % q)
+        gd = gate_columns(ready, T.spay, [("pay", arrival(k, L["pay"][k], core))], 32, 0, T.b0, T.b1, [], [])
+        wd = [("w%d" % f, ways(L["relays"][k][f], L["far_servers"][k])) for f in range(2)]
+        for r in L["order"][core]:
+            i = rl.index(r)
+            d = expert(T.sw, wd, T.tv[:, 256 * i:256 * i + 256], [("tok%d" % i, ways(cores[r], [core]))],
+                       T["b%d" % (2 + 2 * i)], T["b%d" % (3 + 2 * i)], T["b%d" % (6 + i)], i)
+            wait("v", d, gd)
+            d = done("v", V.tensor_tensor(T.rs[:, 256 * i:256 * i + 256], T["b%d" % (6 + i)][:, 0:256], T.gbs[:, 256 * i:256 * i + 256], A.mult))
+            wait("g", d)
+            send([(cores[r], T.rs[:, 256 * k:256 * k + 256])], T.rs[:, 256 * i:256 * i + 256], "res%d" % k)
+        finish()
+        return
+
+    p = L["partner"][rank]
+    foreign = [k for k in range(N) if k not in (rank, p)]
+    first = lambda k: L["order"][L["server"][ch, k]][0] == rank
+    foreign.sort(key=lambda k: (not topo.may_write(cores[k], core), not first(k), k))
+
+    g.sync.dma_start(T.pk[:, :], T.pick[:, :]).then_inc(T.sem.dpick, 16)
+    S.dma_start(T.wo[:, 0:256], T.w1[:, :]).then_inc(T.sem.dw0, 16)
+    S.dma_start(T.wo[:, 256:512], T.w2[:, :]).then_inc(T.sem.dw1, 16)
+    S.dma_start(T.ff[:, 0:8], T.gate[:, :]).then_inc(T.sem.dgate, 16)
+    g.sync.dma_start(T.xs[:, 0:2048], T.x[:, 0:2048]).then_inc(T.sem.dx, 16)
+    g.sync.wait_ge(T.sem.wsent, 1)
+    g.sync.dma_start(T.xs[:, 2048:NT], T.x[:, 2048:NT]).then_inc(T.sem.dx, 16)
+
+    d_one = done("v", V.memset(T.ones[:, :], 1.0))
+    done("v", V.memset(T.c4k[:, :], float(NT)))
+    d_z = done("v", V.memset(T.ys[:, 0:ZC], 0.0))
+    wait("g", d_one)
+    io = lambda out, pat: done("g", g.iota(out, pat, 0, 0, allow_small_or_imprecise_dtypes=True))
+    done("g", g.affine_select(T.tri[:, :], T.ones[:, :], [[1, 128]], A.is_gt, 0.0, 0, -1))
+    io(T.u256[0:1, :], [[0, 8], [256, 8]])
+    d_up = io(T.upat[:, :], [[0, 8], [1, 8]])
+    io(T.iob[:, :], [[0, 8], [1, 16]])
+    io(T.ion[:, :], [[1, 128]])
+    d_cst = io(T.padc[0:1, :], [[0, 8], [16, 16]])
+    wait("s", d_z)
+    for i in range(1, 4):
+        d_zs = done("s", S.activation(T.ys[:, i * ZC:i * ZC + ZC], T.ys[:, 0:ZC], F.Copy))
+    wait("v", d_up)
+    done("v", V.tensor_scalar(T.seg[:, :], T.upat[:, :], 0.0, None, A.is_gt))
+    d_gc = gate_consts([rank])
+
+    for f in range(2):
+        wait("g", ("dw%d" % f, 16))
+        send([(L["relays"][rank][f], T.rlw[:, 256 * f:256 * f + 256])], T.wo[:, 256 * f:256 * f + 256], "rw%d" % f)
+    send([(cores[p], T.sw[:, :])], T.wo[:, :], "w0")
+    g.sem_inc(T.sem.wsent, 1)
+
+    wait("v", ("dpick", 16))
+    d = done("v", V.tensor_scalar(T.rk[:, :], T.pk[:, :], 12, None, A.arith_shift_right))
+    wait("v", d)
+    for u in range(N):
+        d_r = done("v", V.tensor_scalar(T.ror[:, u:64:8], T.rk[:, :], float(u), None, A.is_equal))
+    done("v", V.tensor_scalar(T.tk[:, :], T.pk[:, :], 4095, None, A.bitwise_and))
+    d = done("v", V.tensor_scalar(T.t1[:, :], T.pk[:, :], 4, 1792, A.arith_shift_right, A.bitwise_and))
+    wait("v", d)
+    d = done("v", V.tensor_tensor(T.ds[:, :], T.tk[:, :], T.t1[:, :], A.add))
+    wait("v", d)
+    done("v", V.tensor_scalar(T.dd[:, :], T.ds[:, :], -1.0, float(NT), A.mult, A.add))
+    wait("t", d_r, d_cst)
+    P.matmul(out=T.b0[:, 0:64], lhsT=T.tri[:, :], rhs=T.ror[:, 0:64], start=True, stop=False)
+    for s in range(1, 8):
+        P.matmul(out=T.b0[:, 8 * s:64], lhsT=T.ones[:, :], rhs=T.ror[:, 0:64 - 8 * s], start=False, stop=False)
+    d = done("t", P.matmul(out=T.b0[:, 0:64], lhsT=T.ones[0:1, :], rhs=T.u256[0:1, :], start=False, stop=True))
+    P.matmul(out=T.b1[:, 0:128], lhsT=T.ones[0:1, :], rhs=T.c4k[0:1, :], start=True, stop=False)
+    P.matmul(out=T.b1[:, 0:128], lhsT=T.ones[0:1, :], rhs=T.padc[0:1, :], start=False, stop=False)
+    P.matmul(out=T.b1[:, 0:128], lhsT=T.iob[0:1, :], rhs=T.ones[0:1, :], start=False, stop=False)
+    wait("v", d)
+    d = done("v", V.tensor_tensor(T.rp[:, :], T.b0[:, 0:64], T.ror[:, :], A.mult))
+    wait("v", d)
+    d = done("v", V.tensor_tensor_scan(T.scn[:, :], T.seg[:, :], T.rp[:, :], 0.0, A.mult, A.add))
+    wait("v", d)
+    done("v", V.tensor_copy(T.a32[:, :], T.scn[:, 7:64:8]))
+    d = done("v", V.tensor_tensor(T.v32[:, :], T.scn[:, 7:64:8], T.dd[:, :], A.add))
+    wait("v", d)
+    done("v", V.tensor_scalar(T.ibits[:, 0:8], T.a32[:, :], 15, None, A.bitwise_and))
+    done("v", V.tensor_scalar(T.ibits[:, 8:16], T.a32[:, :], 4, None, A.arith_shift_right))
+    done("v", V.tensor_scalar(T.ibits[:, 16:24], T.v32[:, :], 8128, None, A.bitwise_and))
+    d = done("v", V.tensor_scalar(T.ibits[:, 24:32], T.v32[:, :], 63, None, A.bitwise_and))
+    wait("v", d)
+    d_ff = done("v", V.tensor_copy(T.ff[:, 8:40], T.ibits[:, :]))
+    wait("v", d_ff, d_cst)
+    for m in range(8):
+        a, b = 128 * m, 128 * m + 128
+        done("v", V.tensor_scalar(T.nb[:, a:b], T.iob[:, :], T.ff[:, 8 + m:9 + m], -1.0, A.is_equal, A.mult))
+        done("v", V.tensor_scalar(T.oh[:, a:b], T.ion[:, :], T.ff[:, 16 + m:17 + m], T.ff[:, 24 + m:25 + m], A.is_equal, A.mult))
+        d = done("v", V.tensor_scalar(T.ol[:, a:b], T.ion[:, :], T.ff[:, 16 + m:17 + m], T.ff[:, 32 + m:33 + m], A.is_equal, A.mult))
+        wait("t", d)
+        P.matmul(out=T.b1[:, 0:128], lhsT=T.nb[:, a:b], rhs=T.oh[:, a:b], start=False, stop=False)
+        ins = P.matmul(out=T.b1[:, 0:128], lhsT=T.nb[:, a:b], rhs=T.ol[:, a:b], start=False, stop=m == 7)
+    d = done("t", ins)
+    wait("v", d)
+    d_tab = done("v", V.tensor_copy(T.tabs[:, 128 * rank:128 * rank + 128], T.b1[:, 0:128]))
+
+    wait("g", d_ff, ("dgate", 16))
+    tr = L["trelay"][rank]
+    own = T.tabs[:, 128 * rank:128 * rank + 128]
+    if tr is not None:
+        send([(tr, T.rlp[:, :])], T.ff[:, 0:24], "rpay")
+    send([(c, T.spay[:, :]) for c in split(rank, L["pay"][rank])[0]], T.ff[:, 0:24], "pay")
+    wait("g", d_tab)
+    if tr is not None:
+        send([(tr, T.rlt[:, :])], own, "rtab")
+    send([(c, own) for c in split(rank, L["tab"][rank])[0]], own, "tab%d" % rank)
+
+    wait("v", d_gc)
+    d_ex = done("v", V.tensor_copy(T.expu[:, :], T.expi[:, :]))
+    d_pad = done("v", V.memset(T.xs[:, NT:NX], 0.0))
+    g_own = gate_columns(d_ex, T.ff, [("dgate", 16), d_ff], 16, 0, T.b0, T.b1, [d_tab], [d_tab])
+    g_par = gate_columns(d_ex, T.spay, [("pay", arrival(p, L["pay"][p], core))], 16, 1, T.b0, T.b1, [("cv", count["cv"])], [g_own])
+
+    def table(k):
+        return T.tabs[:, 128 * k + 16 * rank:128 * k + 16 * rank + 16]
+
+    def gather(q, k):
+        wait(q, ("dx", 32), d_pad, d_tab if k == rank else ("tab%d" % k, arrival(k, L["tab"][k], core)))
+        out, src = T.vt[:, 256 * k:256 * k + 256], T.xs[:, :].indirect(table(k))
+        if q == "v":
+            return done("v", V.tensor_copy(out, src))
+        return done("s", S.activation(out, src, F.Copy))
+
+    def deliver(k, d):
+        h = L["server"][ch, k]
+        i = sorted(L["members"][ch]).index(rank)
+        wait("g", d)
+        send([(h, T.tv[:, 256 * i:256 * i + 256])], T.vt[:, 256 * k:256 * k + 256], "tok%d" % i)
+
+    v_own = gather("v", rank)
+    deliver(foreign[0], gather("s", foreign[0]))
+    deliver(foreign[1], gather("v", foreign[1]))
+    deliver(foreign[2], gather("s", foreign[2]))
+    deliver(foreign[3], gather("v", foreign[3]))
+    v_par = gather("s", p)
+    o_own = expert(T.wo, [("dw0", 16), ("dw1", 16)], T.vt[:, 256 * rank:256 * rank + 256], [v_own], T.b2, T.b3, T.b6, 0)
+    deliver(foreign[4], gather("s", foreign[4]))
+    deliver(foreign[5], gather("v", foreign[5]))
+    pw = ("w0", ways(cores[p], [core]))
+    o_par = expert(T.sw, [pw, pw], T.vt[:, 256 * p:256 * p + 256], [v_par], T.b4, T.b5, T.b7, 1)
+
+    def combine(k, deps, start=False):
+        wait("v", *deps)
+        win, res = T.ys[:, :], T.rs[:, 256 * k:256 * k + 256]
+        if not start:
+            wait("v", ("cv", count["cv"]), ("tab%d" % k, arrival(k, L["tab"][k], core)))
+            res = T.tmp[:, :]
+            done("v", V.tensor_tensor(res, win.indirect(table(k)), T.rs[:, 256 * k:256 * k + 256], A.add))
+        wait("v", ("cv", count["cv"]))
+        return done("v", V.tensor_copy(win.indirect(table(k)), res))
+
+    def gated(k, o, bank, i, gd):
+        wait("v", o, gd)
+        return done("v", V.tensor_tensor(T.rs[:, 256 * k:256 * k + 256], bank[:, 0:256], T.gbs[:, 256 * i:256 * i + 256], A.mult))
+
+    combine(rank, [gated(rank, o_own, T.b6, 0, g_own), d_zs], start=True)
+    combine(p, [gated(p, o_par, T.b7, 1, g_par)])
+    foreign.sort(key=lambda k: (not first(k), not topo.may_write(cores[k], core), k))
+    for k in foreign:
+        d = combine(k, [("res%d" % k, ways(L["server"][ch, k], [core]))])
+    wait("d", d)
+    g.sync.dma_start(T.y[:, :], T.ys[:, 0:NT]).then_inc(T.sem.dy, 16)
+    g.sync.wait_ge(T.sem.dy, 16)
+    finish()

@@ -3,7 +3,8 @@ from concourse.mybir import AluOpType as A, ActivationFunctionType as F
 
 N, NT, CP = 8, 4096, 256
 NX = NT + CP
-ZC = NX // 4
+ZC = NX // 16
+X1 = 2048
 
 SCRATCH = {
     "pk": ("sbuf", [128, 8], "int32"), "rk": ("sbuf", [128, 8], "int32"), "tk": ("sbuf", [128, 8], "int32"),
@@ -17,22 +18,23 @@ SCRATCH = {
     "iob": ("sbuf", [128, 128], "bfloat16"), "ion": ("sbuf", [128, 128], "bfloat16"),
     "padc": ("sbuf", [128, 128], "bfloat16"), "c4k": ("sbuf", [128, 128], "bfloat16"), "u256": ("sbuf", [128, 64], "bfloat16"),
     "upat": ("sbuf", [128, 64], "float32"), "seg": ("sbuf", [128, 64], "float32"),
-    "onesf": ("sbuf", [128, 512], "float32"), "diag": ("sbuf", [128, 512], "float32"),
-    "iobf": ("sbuf", [128, 128], "float32"), "iorc": ("sbuf", [128, 32], "float32"),
-    "expi": ("sbuf", [128, 32], "int32"), "expu": ("sbuf", [128, 32], "uint16"),
-    "spay": ("sbuf", [128, 24], "float32"),
-    "gob": ("sbuf", [128, 2048], "float32"), "gor": ("sbuf", [128, 512], "float32"),
-    "gws": ("sbuf", [128, 64], "float32"), "gx": ("sbuf", [128, 512], "float32"), "gbs": ("sbuf", [128, 512], "float32"),
+    "ip": ("sbuf", [128, 4], "int32"), "ic": ("sbuf", [128, 4], "int32"), "ih": ("sbuf", [128, 4], "int32"),
+    "e8i": ("sbuf", [128, 4], "int32"), "e8": ("sbuf", [128, 4], "uint16"),
+    "onesf": ("sbuf", [128, 256], "float32"), "diag": ("sbuf", [128, 256], "float32"),
+    "iobf": ("sbuf", [128, 128], "float32"), "iorc": ("sbuf", [128, 256], "float32"),
+    "expi": ("sbuf", [128, 16], "int32"), "expu": ("sbuf", [128, 16], "uint16"),
+    "spay": ("sbuf", [128, 24], "float32"), "rlp": ("sbuf", [128, 24], "float32"),
+    "gob": ("sbuf", [128, 256], "float32"), "goc": ("sbuf", [128, 256], "float32"), "gor": ("sbuf", [128, 256], "float32"),
+    "gws": ("sbuf", [128, 32], "float32"), "gx": ("sbuf", [128, 512], "float32"), "gbs": ("sbuf", [128, 512], "float32"),
     "wo": ("sbuf", [128, 512], "float32"), "sw": ("sbuf", [128, 512], "float32"), "rlw": ("sbuf", [128, 512], "float32"),
-    "rlp": ("sbuf", [128, 24], "float32"), "rlt": ("sbuf", [128, 128], "uint16"),
     "xs": ("sbuf", [128, NX], "float32"), "ys": ("sbuf", [128, NX], "float32"),
     "vt": ("sbuf", [128, 2048], "float32"), "tv": ("sbuf", [128, 512], "float32"),
     "hs": ("sbuf", [128, 1024], "float32"), "rs": ("sbuf", [128, 2048], "float32"), "tmp": ("sbuf", [128, 256], "float32"),
 }
 for _i in range(8):
     SCRATCH["b%d" % _i] = ("psum", [128, 512], "float32")
-SEMAPHORES = (["cg", "cv", "cs", "ct", "loc", "wsent", "dpick", "dgate", "dw0", "dw1", "dx", "dy", "pay", "w0", "w1",
-               "rw0", "rw1", "rpay", "rtab", "tok0", "tok1"]
+SEMAPHORES = (["cg", "cv", "cs", "ct", "loc", "wsent", "dpick", "dgate", "dw0", "dw1", "dx", "dy", "pay", "rpay", "w0", "w1",
+               "rw0", "rw1", "tok0", "tok1"]
               + ["tab%d" % k for k in range(N)] + ["res%d" % k for k in range(N)])
 
 
@@ -48,15 +50,15 @@ def layout(T, topo):
         return all(topo.may_write(c, d) for d in cores if d != c)
 
     members = {ch: [k for k in range(N) if topo.chip(cores[k]) == ch] for ch in chips}
+    partner = {k: [q for q in members[topo.chip(cores[k])] if q != k][0] for k in range(N)}
     helpers = {ch: [c for c in every if topo.chip(c) == ch and c not in cores] for ch in chips}
-    relays, trelay = {}, {}
+    relays = {}
     for k in range(N):
         ports = [h for h in helpers[topo.chip(cores[k])] if free(h)]
         near = [h for h in ports if topo.die(h) == topo.die(cores[k])]
         far = [h for h in ports if topo.die(h) != topo.die(cores[k])]
         use = (near or far) if free(cores[k]) else (far or near)
         relays[k] = [use[0], use[-1]]
-        trelay[k] = None if free(cores[k]) else (near or far)[0]
     server, serves = {}, {}
     for ch in chips:
         left = list(helpers[ch])
@@ -68,17 +70,14 @@ def layout(T, topo):
             server[ch, k] = h
             serves[h] = k
     far_servers = {k: [server[ch, k] for ch in chips if ch != topo.chip(cores[k])] for k in range(N)}
-    partner = {k: [q for q in members[topo.chip(cores[k])] if q != k][0] for k in range(N)}
-    pay = {k: [cores[partner[k]]] + far_servers[k] for k in range(N)}
-    tab = {k: [cores[q] for q in range(N) if q != k] for k in range(N)}
+    tab = {k: [cores[q] for q in range(N) if q not in (k, partner[k])] for k in range(N)}
     order = {}
     for ch in chips:
         for i, h in enumerate(helpers[ch]):
             m = members[ch]
             order[h] = m if i % 2 == 0 else m[::-1]
-    return {"cores": cores, "chips": chips, "members": members, "helpers": helpers, "relays": relays, "trelay": trelay,
-            "server": server, "serves": serves, "far_servers": far_servers, "partner": partner, "pay": pay, "tab": tab,
-            "order": order}
+    return {"cores": cores, "chips": chips, "members": members, "relays": relays, "server": server, "serves": serves,
+            "pay": far_servers, "partner": partner, "tab": tab, "order": order}
 
 
 def rank_program(g, core, T, topo):
@@ -88,6 +87,7 @@ def rank_program(g, core, T, topo):
     if ch not in L["chips"]:
         return
     rank = T.rank_of(core)
+    pair = L["members"][ch]
     Q = {"g": g, "v": g.vector, "s": g.scalar, "t": g.tensor, "d": g.sync}
     V, S, P = g.vector, g.scalar, g.tensor
     count, seen = {"loc": 0}, {}
@@ -104,73 +104,106 @@ def rank_program(g, core, T, topo):
         ins.then_inc(T.sem[name], 1)
         return (name, count[name])
 
-    def engines(src, dsts):
+    def engines(src, dsts, i=0, n=1):
         m = topo.mask(src, dsts[0])
         for d in dsts[1:]:
             m &= topo.mask(src, d)
-        return m
+        bits = [b for b in range(m.bit_length()) if m >> b & 1][i::n]
+        return sum(1 << b for b in bits)
 
-    def ways(src, dsts):
-        return bin(engines(src, dsts)).count("1")
+    def inner(src, dst):
+        return topo.mask(src, dst) & ~topo.mask(src, [c for c in cores if topo.chip(c) != topo.chip(src)][0])
 
-    def send(targets, src_ap, rsem):
-        m = engines(core, [c for c, ap in targets])
-        if len(targets) == 1:
-            rid, pid, se = topo.addr(targets[0][0])
-            g.remote_dma(out_ap=targets[0][1], in_ap=src_ap, remote_sem=T.sem[rsem], local_sem=T.sem.loc, pid=pid,
-                         routing_id=rid, dma_engine_mask=m)
-        else:
+    def ways(src, dsts, i=0, n=1):
+        return bin(engines(src, dsts, i, n)).count("1")
+
+    def send(*transfers):
+        n, out = len(transfers), []
+        for i, (targets, src, rsem, *own) in enumerate(transfers):
+            m = own[0] if own else engines(core, [c for c, ap in targets], i, n)
+            count["loc"] += bin(m).count("1")
             ids = []
             for c, ap in targets:
                 rid, pid, se = topo.addr(c)
                 ids.append(DstId(rid=rid, pnc=pid))
-            g.remote_dma_fused([RemoteDMATransfer(dst_ids=ids, dma_engine_mask=m, remote_sem=T.sem[rsem], srcs=[src_ap],
-                                                  dsts=[ap for c, ap in targets])], local_sem=T.sem.loc)
-        count["loc"] += bin(m).count("1")
+            if n == 1 and len(targets) == 1:
+                g.remote_dma(out_ap=targets[0][1], in_ap=src, remote_sem=T.sem[rsem], local_sem=T.sem.loc, pid=pid,
+                             routing_id=rid, dma_engine_mask=m)
+                return
+            out.append(RemoteDMATransfer(dst_ids=ids, dma_engine_mask=m, remote_sem=T.sem[rsem], srcs=[src],
+                                         dsts=[ap for c, ap in targets]))
+        g.remote_dma_fused(out, local_sem=T.sem.loc)
 
-    def split(k, dsts):
-        direct = [d for d in dsts if topo.may_write(cores[k], d)]
-        return direct, [d for d in dsts if d not in direct]
+    def direct(k, dsts):
+        return [d for d in dsts if topo.may_write(cores[k], d)]
 
-    def arrival(k, dsts, me):
-        direct, rest = split(k, dsts)
-        return ways(cores[k], direct) if me in direct else ways(L["trelay"][k], rest)
+    def passed(k, dsts):
+        far = [c for c in L["chips"] if not topo.may_write(cores[k], cores[L["members"][c][0]])]
+        out = {}
+        for d in dsts:
+            if not topo.may_write(cores[k], d):
+                out.setdefault(L["relays"][k][far.index(topo.chip(d)) % 2], []).append(d)
+        return out
 
-    def gate_consts(rl):
-        n = 16 * len(rl)
-        d1 = done("v", V.memset(T.onesf[:, 0:512], 1.0))
-        done("g", g.iota(T.iobf[:, :], [[0, 8], [1, 16]], 0, 0, allow_small_or_imprecise_dtypes=True))
-        step = 16 * (rl[-1] - rl[0])
-        done("g", g.iota(T.iorc[:, 0:n], [[step, len(rl)], [1, 16]], 16 * rl[0], 0, allow_small_or_imprecise_dtypes=True))
-        done("g", g.iota(T.expi[:, :], [[1, 32]], 0, 0))
+    def arrival(k, dsts, to):
+        if topo.chip(to) == topo.chip(cores[k]):
+            return bin(inner(cores[k], to)).count("1")
+        for q, ds in passed(k, dsts).items():
+            if to in ds:
+                return ways(q, ds)
+        return ways(cores[k], direct(k, dsts))
+
+    def share(k, dsts, place0, sem0, place, sem, src):
+        near = [cores[L["partner"][k]]] + list(passed(k, dsts))
+        send(([(c, place0) for c in near], src, sem0, inner(core, near[0])),
+             ([(c, place) for c in direct(k, dsts)], src, sem, engines(core, direct(k, dsts))))
+
+    def io(out, pat, base=0, cm=0):
+        return done("g", g.iota(out, pat, base, cm, allow_small_or_imprecise_dtypes=True))
+
+    def gate_fills():
+        return done("v", V.memset(T.gws[:, :], 0.0)), done("v", V.memset(T.onesf[:, :], 1.0))
+
+    def gate_consts(rl, d0, d1):
+        io(T.iobf[:, :], [[0, 8], [1, 16]])
+        for i, r in enumerate(rl):
+            io(T.iorc[:, 128 * i:128 * i + 128], [[0, 8], [1, 16]], 16 * r)
+        done("g", g.iota(T.expi[:, :], [[1, 16]], 0, 0))
         wait("g", d1)
-        return done("g", g.affine_select(T.diag[:, 0:16 * n], T.onesf[:, 0:16 * n], [[0, n], [1, 16]], A.is_equal, 0.0, 0, -1))
+        wait("s", d0)
+        return done("g", g.affine_select(T.diag[:, :], T.onesf[:, :], [[0, 16], [1, 16]], A.is_equal, 0.0, 0, -1))
 
-    def gate_columns(ready, pay, pdeps, n, i, gw, gb, free_gw, free_gb):
-        wait("v", ready, *pdeps)
-        ob, orc, dl = 1024 * i, 256 * i, []
-        for m in range(8):
-            done("v", V.tensor_scalar(T.gob[:, ob + 128 * m:ob + 128 * m + 128], T.iobf[:, :], pay[:, 8 + m:9 + m], None, A.is_equal))
-            dl.append(done("v", V.tensor_scalar(T.gor[:, orc + n * m:orc + n * m + n], T.iorc[:, 0:n], pay[:, 16 + m:17 + m],
-                                                pay[:, m:m + 1], A.is_equal, A.mult)))
-        wait("t", *free_gw)
-        for m in range(8):
-            wait("t", dl[m])
-            ins = P.matmul(out=gw[:, 0:n], lhsT=T.gob[:, ob + 128 * m:ob + 128 * m + 128], rhs=T.gor[:, orc + n * m:orc + n * m + n],
-                           start=m == 0, stop=m == 7)
-        d = done("t", ins)
+    def gate_hots(pay, i, c):
+        a, b = 128 * i, 128 * i + 128
+        d = done("v", V.tensor_tensor(T.goc[:, a:b], pay[:, 16:24].indirect(T.expu[:, 0:8]), T.iorc[:, 128 * c:128 * c + 128], A.is_equal))
+        done("v", V.tensor_tensor(T.gob[:, a:b], pay[:, 8:16].indirect(T.expu[:, 0:8]), T.iobf[:, :], A.is_equal))
         wait("v", d)
-        d = done("v", V.tensor_copy(T.gws[:, 32 * i:32 * i + n], gw[:, 0:n]))
+        return done("v", V.tensor_tensor(T.gor[:, a:b], pay[:, 0:8].indirect(T.expu[:, 0:8]), T.goc[:, a:b], A.mult))
+
+    def gate_table(d, i, bank, *free):
+        wait("t", d, *free)
+        for m in range(8):
+            a = 128 * i + 16 * m
+            ins = P.matmul(out=bank[0:16, 0:16], lhsT=T.gob[:, a:a + 16], rhs=T.gor[:, a:a + 16], start=m == 0, stop=m == 7)
+        return done("t", ins)
+
+    def gate_row(d, i, bank):
+        wait("s", d)
+        return done("s", S.activation(T.gws[0:16, 16 * i:16 * i + 16], bank[0:16, 0:16], F.Copy))
+
+    def spread_rows(d, i):
         wait("v", d)
         c = 256 * i
-        d = done("v", V.tensor_tensor(T.gx[:, c:c + 16 * n], T.gws[:, 32 * i:32 * i + n].indirect(T.expu[:, 0:n]),
-                                      T.diag[:, 0:16 * n], A.mult))
-        wait("t", d, *free_gb)
-        d = done("t", P.matmul(out=gb[:, 0:16 * n], lhsT=T.onesf[0:16, 0:128], rhs=T.gx[0:16, c:c + 16 * n], start=True, stop=True))
-        wait("s", d)
-        return done("s", S.activation(T.gbs[:, c:c + 16 * n], gb[:, 0:16 * n], F.Copy))
+        return done("v", V.tensor_tensor(T.gx[:, c:c + 256], T.gws[:, 16 * i:16 * i + 16].indirect(T.expu[:, :]), T.diag[:, :], A.mult))
 
-    def expert(w, wdeps, rhs, rdeps, h0, h1, ob, i):
+    def spread_all(d, i, bank, *free):
+        c = 256 * i
+        wait("t", d, *free)
+        d = done("t", P.matmul(out=bank[:, 0:256], lhsT=T.onesf[0:16, 0:128], rhs=T.gx[0:16, c:c + 256], start=True, stop=True))
+        wait("s", d)
+        return done("s", S.activation(T.gbs[:, c:c + 256], bank[:, 0:256], F.Copy))
+
+    def expert(w, wdeps, rhs, rdeps, h0, h1, ob, i, between=None):
         wait("t", wdeps[0], *rdeps)
         hp, c, e = [h0, h1], [], []
         for f in range(2):
@@ -179,12 +212,17 @@ def rank_program(g, core, T, topo):
             a = 512 * i + 256 * f
             wait("s", c[f])
             e.append(done("s", S.activation(T.hs[:, a:a + 256], hp[f][:, 0:256], F.Relu)))
+        mid = between() if between else None
         wait("t", wdeps[1])
         for f in range(2):
             a = 512 * i + 256 * f
             wait("t", e[f])
             ins = P.matmul(out=ob[:, 0:256], lhsT=w[:, 256 + 128 * f:384 + 128 * f], rhs=T.hs[:, a:a + 256], start=f == 0, stop=f == 1)
-        return done("t", ins)
+        return done("t", ins), mid
+
+    def gated(i, o, bank, gd, out):
+        wait("v", o, gd)
+        return done("v", V.tensor_tensor(out, bank[:, 0:256], T.gbs[:, 256 * i:256 * i + 256], A.mult))
 
     def finish():
         for name in ("cg", "cv", "cs", "ct", "loc"):
@@ -193,76 +231,83 @@ def rank_program(g, core, T, topo):
 
     if rank is None:
         k = L["serves"][core]
-        rl = sorted(L["members"][ch])
-        ready = gate_consts(rl)
-        wait("v", ready)
-        ready = done("v", V.tensor_copy(T.expu[:, :], T.expi[:, :]))
+        wait("v", gate_consts(pair, *gate_fills()))
+        d = done("v", V.tensor_copy(T.expu[:, :], T.expi[:, :]))
         for f in range(2):
-            for q in L["members"][ch]:
+            for q in pair:
                 if L["relays"][q][f] == core:
-                    wait("g", ("rw%d" % f, ways(cores[q], [core])))
-                    send([(h, T.sw[:, 256 * f:256 * f + 256]) for h in L["far_servers"][q]], T.rlw[:, 256 * f:256 * f + 256], "w%d" % f)
-        for q in L["members"][ch]:
-            if L["trelay"][q] == core:
-                wait("g", ("rpay", ways(cores[q], [core])))
-                send([(h, T.spay[:, :]) for h in split(q, L["pay"][q])[1]], T.rlp[:, :], "pay")
-                wait("g", ("rtab", ways(cores[q], [core])))
-                send([(c, T.tabs[:, 128 * q:128 * q + 128]) for c in split(q, L["tab"][q])[1]], T.rlt[:, :], "tab%d" % q)
-        gd = gate_columns(ready, T.spay, [("pay", arrival(k, L["pay"][k], core))], 32, 0, T.b0, T.b1, [], [])
-        wd = [("w%d" % f, ways(L["relays"][k][f], L["far_servers"][k])) for f in range(2)]
+                    wait("g", ("rw%d" % f, ways(cores[q], [core], f, 2)))
+                    send(([(h, T.sw[:, 256 * f:256 * f + 256]) for h in L["pay"][q]], T.rlw[:, 256 * f:256 * f + 256], "w%d" % f))
+        for q in pair:
+            if core in passed(q, L["pay"][q]):
+                wait("g", ("rpay", arrival(q, L["pay"][q], core)))
+                send(([(c, T.spay[:, :]) for c in passed(q, L["pay"][q])[core]], T.rlp[:, :], "pay"))
+                col = T.tabs[:, 128 * q:128 * q + 128]
+                wait("g", ("tab%d" % q, arrival(q, L["tab"][q], core)))
+                send(([(c, col) for c in passed(q, L["tab"][q])[core]], col, "tab%d" % q))
+        wait("v", d, ("pay", arrival(k, L["pay"][k], core)))
+        hots = [gate_hots(T.spay, i, i) for i in range(2)]
+        rows = [gate_table(hots[i], i, T["b%d" % i]) for i in range(2)]
+        rows = [gate_row(rows[i], i, T["b%d" % i]) for i in range(2)]
+        gd = [spread_all(spread_rows(rows[i], i), i, T["b%d" % i], rows[i]) for i in range(2)]
+        wd = [("w%d" % f, ways(L["relays"][k][f], L["pay"][k])) for f in range(2)]
         for r in L["order"][core]:
-            i = rl.index(r)
-            d = expert(T.sw, wd, T.tv[:, 256 * i:256 * i + 256], [("tok%d" % i, ways(cores[r], [core]))],
-                       T["b%d" % (2 + 2 * i)], T["b%d" % (3 + 2 * i)], T["b%d" % (6 + i)], i)
-            wait("v", d, gd)
-            d = done("v", V.tensor_tensor(T.rs[:, 256 * i:256 * i + 256], T["b%d" % (6 + i)][:, 0:256], T.gbs[:, 256 * i:256 * i + 256], A.mult))
-            wait("g", d)
-            send([(cores[r], T.rs[:, 256 * k:256 * k + 256])], T.rs[:, 256 * i:256 * i + 256], "res%d" % k)
+            i = pair.index(r)
+            ob, res = T["b%d" % (6 + i)], T.rs[:, 256 * i:256 * i + 256]
+            d, _ = expert(T.sw, wd, T.tv[:, 256 * i:256 * i + 256], [("tok%d" % i, ways(cores[r], [core], 0, 2))],
+                          T["b%d" % (2 + 2 * i)], T["b%d" % (3 + 2 * i)], ob, i)
+            wait("g", gated(i, d, ob, gd[i], res))
+            send(([(cores[r], T.rs[:, 256 * k:256 * k + 256])], res, "res%d" % k))
         finish()
         return
 
     p = L["partner"][rank]
-    foreign = [k for k in range(N) if k not in (rank, p)]
+    me = pair.index(rank)
+    foreign = [k for k in range(N) if k not in pair]
     first = lambda k: L["order"][L["server"][ch, k]][0] == rank
-    foreign.sort(key=lambda k: (not topo.may_write(cores[k], core), not first(k), k))
+    slow = lambda k: not topo.may_write(cores[k], core)
+    foreign.sort(key=lambda k: (slow(k), not first(k), k))
 
     g.sync.dma_start(T.pk[:, :], T.pick[:, :]).then_inc(T.sem.dpick, 16)
+    g.sync.dma_start(T.ff[:, 0:8], T.gate[:, :]).then_inc(T.sem.dgate, 16)
     S.dma_start(T.wo[:, 0:256], T.w1[:, :]).then_inc(T.sem.dw0, 16)
     S.dma_start(T.wo[:, 256:512], T.w2[:, :]).then_inc(T.sem.dw1, 16)
-    S.dma_start(T.ff[:, 0:8], T.gate[:, :]).then_inc(T.sem.dgate, 16)
-    g.sync.dma_start(T.xs[:, 0:2048], T.x[:, 0:2048]).then_inc(T.sem.dx, 16)
+    g.sync.dma_start(T.xs[:, 0:X1], T.x[:, 0:X1]).then_inc(T.sem.dx, 16)
     g.sync.wait_ge(T.sem.wsent, 1)
-    g.sync.dma_start(T.xs[:, 2048:NT], T.x[:, 2048:NT]).then_inc(T.sem.dx, 16)
+    g.sync.dma_start(T.xs[:, X1:NT], T.x[:, X1:NT]).then_inc(T.sem.dx, 16)
 
-    d_one = done("v", V.memset(T.ones[:, :], 1.0))
-    done("v", V.memset(T.c4k[:, :], float(NT)))
-    d_z = done("v", V.memset(T.ys[:, 0:ZC], 0.0))
-    wait("g", d_one)
-    io = lambda out, pat: done("g", g.iota(out, pat, 0, 0, allow_small_or_imprecise_dtypes=True))
-    done("g", g.affine_select(T.tri[:, :], T.ones[:, :], [[1, 128]], A.is_gt, 0.0, 0, -1))
-    io(T.u256[0:1, :], [[0, 8], [256, 8]])
+    done("g", g.iota(T.ip[:, :], [[0, 4]], 0, 1))
+    d_e8 = done("g", g.iota(T.ic[:, :], [[2, 4]], 0, 0))
     d_up = io(T.upat[:, :], [[0, 8], [1, 8]])
+    io(T.u256[0:1, :], [[0, 8], [256, 8]])
+    d_one = done("v", V.memset(T.ones[:, :], 1.0))
+    d_zs = done("v", V.memset(T.ys[:, 0:ZC], 0.0))
+    done("v", V.memset(T.c4k[0:1, :], float(NT)))
+    wait("v", d_e8)
+    d = done("v", V.tensor_scalar(T.ih[:, :], T.ip[:, :], 3, 1, A.arith_shift_right, A.bitwise_and))
+    wait("v", d)
+    d = done("v", V.tensor_tensor(T.e8i[:, :], T.ih[:, :], T.ic[:, :], A.add))
+    wait("v", d, d_up)
+    done("v", V.tensor_copy(T.e8[:, :], T.e8i[:, :]))
+    d_seg = done("v", V.tensor_scalar(T.seg[:, :], T.upat[:, :], 0.0, None, A.is_gt))
+    fills = gate_fills()
+    wait("g", d_one)
+    done("g", g.affine_select(T.tri[:, :], T.ones[:, :], [[1, 128]], A.is_gt, 0.0, 0, -1))
     io(T.iob[:, :], [[0, 8], [1, 16]])
     io(T.ion[:, :], [[1, 128]])
     d_cst = io(T.padc[0:1, :], [[0, 8], [16, 16]])
-    wait("s", d_z)
-    for i in range(1, 4):
-        d_zs = done("s", S.activation(T.ys[:, i * ZC:i * ZC + ZC], T.ys[:, 0:ZC], F.Copy))
-    wait("v", d_up)
-    done("v", V.tensor_scalar(T.seg[:, :], T.upat[:, :], 0.0, None, A.is_gt))
-    d_gc = gate_consts([rank])
+    for i in range(4):
+        wait("s", d_zs)
+        d_zs = done("s", S.activation(T.ys[:, ZC << i:ZC << i + 1], T.ys[:, 0:ZC << i], F.Copy))
 
-    for f in range(2):
-        wait("g", ("dw%d" % f, 16))
-        send([(L["relays"][rank][f], T.rlw[:, 256 * f:256 * f + 256])], T.wo[:, 256 * f:256 * f + 256], "rw%d" % f)
-    send([(cores[p], T.sw[:, :])], T.wo[:, :], "w0")
+    wait("g", ("dw0", 16), ("dw1", 16))
+    send(*[([(L["relays"][rank][f], T.rlw[:, 256 * f:256 * f + 256])], T.wo[:, 256 * f:256 * f + 256], "rw%d" % f) for f in range(2)])
     g.sem_inc(T.sem.wsent, 1)
 
     wait("v", ("dpick", 16))
     d = done("v", V.tensor_scalar(T.rk[:, :], T.pk[:, :], 12, None, A.arith_shift_right))
-    wait("v", d)
-    for u in range(N):
-        d_r = done("v", V.tensor_scalar(T.ror[:, u:64:8], T.rk[:, :], float(u), None, A.is_equal))
+    wait("v", d, d_seg)
+    d_r = done("v", V.tensor_tensor(T.ror[:, :], T.rk[:, :].indirect(T.e8[:, :]), T.upat[:, :], A.is_equal))
     done("v", V.tensor_scalar(T.tk[:, :], T.pk[:, :], 4095, None, A.bitwise_and))
     d = done("v", V.tensor_scalar(T.t1[:, :], T.pk[:, :], 4, 1792, A.arith_shift_right, A.bitwise_and))
     wait("v", d)
@@ -282,19 +327,24 @@ def rank_program(g, core, T, topo):
     wait("v", d)
     d = done("v", V.tensor_tensor_scan(T.scn[:, :], T.seg[:, :], T.rp[:, :], 0.0, A.mult, A.add))
     wait("v", d)
-    done("v", V.tensor_copy(T.a32[:, :], T.scn[:, 7:64:8]))
-    d = done("v", V.tensor_tensor(T.v32[:, :], T.scn[:, 7:64:8], T.dd[:, :], A.add))
-    wait("v", d)
+    d_a = done("v", V.tensor_copy(T.a32[:, :], T.scn[:, 7:64:8]))
+    d_v = done("v", V.tensor_tensor(T.v32[:, :], T.scn[:, 7:64:8], T.dd[:, :], A.add))
+    wait("v", d_a)
     done("v", V.tensor_scalar(T.ibits[:, 0:8], T.a32[:, :], 15, None, A.bitwise_and))
-    done("v", V.tensor_scalar(T.ibits[:, 8:16], T.a32[:, :], 4, None, A.arith_shift_right))
+    d_a = done("v", V.tensor_scalar(T.ibits[:, 8:16], T.a32[:, :], 4, None, A.arith_shift_right))
+    wait("v", d_v)
     done("v", V.tensor_scalar(T.ibits[:, 16:24], T.v32[:, :], 8128, None, A.bitwise_and))
-    d = done("v", V.tensor_scalar(T.ibits[:, 24:32], T.v32[:, :], 63, None, A.bitwise_and))
-    wait("v", d)
-    d_ff = done("v", V.tensor_copy(T.ff[:, 8:40], T.ibits[:, :]))
+    d_v = done("v", V.tensor_scalar(T.ibits[:, 24:32], T.v32[:, :], 63, None, A.bitwise_and))
+    wait("v", d_a)
+    d_ff = done("v", V.tensor_copy(T.ff[:, 8:24], T.ibits[:, 0:16]))
+    wait("v", d_v)
+    d_fv = done("v", V.tensor_copy(T.ff[:, 24:40], T.ibits[:, 16:32]))
     wait("v", d_ff, d_cst)
     for m in range(8):
+        done("v", V.tensor_scalar(T.nb[:, 128 * m:128 * m + 128], T.iob[:, :], T.ff[:, 8 + m:9 + m], -1.0, A.is_equal, A.mult))
+    wait("v", d_fv)
+    for m in range(8):
         a, b = 128 * m, 128 * m + 128
-        done("v", V.tensor_scalar(T.nb[:, a:b], T.iob[:, :], T.ff[:, 8 + m:9 + m], -1.0, A.is_equal, A.mult))
         done("v", V.tensor_scalar(T.oh[:, a:b], T.ion[:, :], T.ff[:, 16 + m:17 + m], T.ff[:, 24 + m:25 + m], A.is_equal, A.mult))
         d = done("v", V.tensor_scalar(T.ol[:, a:b], T.ion[:, :], T.ff[:, 16 + m:17 + m], T.ff[:, 32 + m:33 + m], A.is_equal, A.mult))
         wait("t", d)
@@ -304,70 +354,70 @@ def rank_program(g, core, T, topo):
     wait("v", d)
     d_tab = done("v", V.tensor_copy(T.tabs[:, 128 * rank:128 * rank + 128], T.b1[:, 0:128]))
 
+    col = T.tabs[:, 128 * rank:128 * rank + 128]
     wait("g", d_ff, ("dgate", 16))
-    tr = L["trelay"][rank]
-    own = T.tabs[:, 128 * rank:128 * rank + 128]
-    if tr is not None:
-        send([(tr, T.rlp[:, :])], T.ff[:, 0:24], "rpay")
-    send([(c, T.spay[:, :]) for c in split(rank, L["pay"][rank])[0]], T.ff[:, 0:24], "pay")
+    share(rank, L["pay"][rank], T.rlp[:, :], "rpay", T.spay[:, :], "pay", T.ff[:, 0:24])
+    d_gc = gate_consts([rank], *fills)
     wait("g", d_tab)
-    if tr is not None:
-        send([(tr, T.rlt[:, :])], own, "rtab")
-    send([(c, own) for c in split(rank, L["tab"][rank])[0]], own, "tab%d" % rank)
+    share(rank, L["tab"][rank], col, "tab%d" % rank, col, "tab%d" % rank, col)
+    send(([(cores[p], T.sw[:, :])], T.wo[:, :], "w0"))
 
-    wait("v", d_gc)
-    d_ex = done("v", V.tensor_copy(T.expu[:, :], T.expi[:, :]))
     d_pad = done("v", V.memset(T.xs[:, NT:NX], 0.0))
-    g_own = gate_columns(d_ex, T.ff, [("dgate", 16), d_ff], 16, 0, T.b0, T.b1, [d_tab], [d_tab])
-    g_par = gate_columns(d_ex, T.spay, [("pay", arrival(p, L["pay"][p], core))], 16, 1, T.b0, T.b1, [("cv", count["cv"])], [g_own])
+    wait("v", d_gc)
+    d = done("v", V.tensor_copy(T.expu[:, :], T.expi[:, :]))
+    wait("v", d, ("dgate", 16))
+    h_own = gate_hots(T.ff, 0, 0)
+    wait("v", ("rpay", arrival(p, L["pay"][p], core)))
+    h_par = gate_hots(T.rlp, 1, 0)
 
     def table(k):
-        return T.tabs[:, 128 * k + 16 * rank:128 * k + 16 * rank + 16]
+        return d_tab if k == rank else ("tab%d" % k, arrival(k, L["tab"][k], core))
 
     def gather(q, k):
-        wait(q, ("dx", 32), d_pad, d_tab if k == rank else ("tab%d" % k, arrival(k, L["tab"][k], core)))
-        out, src = T.vt[:, 256 * k:256 * k + 256], T.xs[:, :].indirect(table(k))
+        wait(q, ("dx", 32), d_pad, table(k))
+        c = 128 * k + 16 * rank
+        out, src = T.vt[:, 256 * k:256 * k + 256], T.xs[:, :].indirect(T.tabs[:, c:c + 16])
         if q == "v":
             return done("v", V.tensor_copy(out, src))
         return done("s", S.activation(out, src, F.Copy))
 
-    def deliver(k, d):
-        h = L["server"][ch, k]
-        i = sorted(L["members"][ch]).index(rank)
-        wait("g", d)
-        send([(h, T.tv[:, 256 * i:256 * i + 256])], T.vt[:, 256 * k:256 * k + 256], "tok%d" % i)
+    def deliver(ks, *deps):
+        wait("g", *deps)
+        send(*[([(L["server"][ch, k], T.tv[:, 256 * me:256 * me + 256])], T.vt[:, 256 * k:256 * k + 256], "tok%d" % me) for k in ks])
 
-    v_own = gather("v", rank)
-    deliver(foreign[0], gather("s", foreign[0]))
-    deliver(foreign[1], gather("v", foreign[1]))
-    deliver(foreign[2], gather("s", foreign[2]))
-    deliver(foreign[3], gather("v", foreign[3]))
+    v_own = gather("s", rank)
+    o_own, _ = expert(T.wo, [("dw0", 16), ("dw1", 16)], T.vt[:, 256 * rank:256 * rank + 256], [v_own], T.b2, T.b3, T.b6, 0)
+    deliver(foreign[0:2], gather("s", foreign[0]), gather("v", foreign[1]))
+    deliver(foreign[2:4], gather("s", foreign[2]), gather("v", foreign[3]))
     v_par = gather("s", p)
-    o_own = expert(T.wo, [("dw0", 16), ("dw1", 16)], T.vt[:, 256 * rank:256 * rank + 256], [v_own], T.b2, T.b3, T.b6, 0)
-    deliver(foreign[4], gather("s", foreign[4]))
-    deliver(foreign[5], gather("v", foreign[5]))
+    t_own, t_par = gate_table(h_own, 0, T.b0, d_tab), gate_table(h_par, 1, T.b1, d_tab)
+    r_own = gate_row(t_own, 0, T.b0)
+    m_own = spread_rows(r_own, 0)
+    r_par = gate_row(t_par, 1, T.b1)
+    g_own = spread_all(m_own, 0, T.b0, r_own)
+    deliver(foreign[4:6], gather("v", foreign[4]), gather("v", foreign[5]))
+    m_par = spread_rows(r_par, 1)
     pw = ("w0", ways(cores[p], [core]))
-    o_par = expert(T.sw, [pw, pw], T.vt[:, 256 * p:256 * p + 256], [v_par], T.b4, T.b5, T.b7, 1)
+    o_par, g_par = expert(T.sw, [pw, pw], T.vt[:, 256 * p:256 * p + 256], [v_par], T.b4, T.b5, T.b7, 1,
+                          lambda: spread_all(m_par, 1, T.b1, r_par))
 
-    def combine(k, deps, start=False):
-        wait("v", *deps)
+    def combine(k, dep, start=False):
+        wait("v", dep)
         win, res = T.ys[:, :], T.rs[:, 256 * k:256 * k + 256]
+        c = 128 * k + 16 * rank
+        off = T.tabs[:, c:c + 16]
         if not start:
-            wait("v", ("cv", count["cv"]), ("tab%d" % k, arrival(k, L["tab"][k], core)))
+            wait("v", ("cv", count["cv"]), table(k))
+            done("v", V.tensor_tensor(T.tmp[:, :], win.indirect(off), res, A.add))
             res = T.tmp[:, :]
-            done("v", V.tensor_tensor(res, win.indirect(table(k)), T.rs[:, 256 * k:256 * k + 256], A.add))
         wait("v", ("cv", count["cv"]))
-        return done("v", V.tensor_copy(win.indirect(table(k)), res))
+        return done("v", V.tensor_copy(win.indirect(off), res))
 
-    def gated(k, o, bank, i, gd):
-        wait("v", o, gd)
-        return done("v", V.tensor_tensor(T.rs[:, 256 * k:256 * k + 256], bank[:, 0:256], T.gbs[:, 256 * i:256 * i + 256], A.mult))
-
-    combine(rank, [gated(rank, o_own, T.b6, 0, g_own), d_zs], start=True)
-    combine(p, [gated(p, o_par, T.b7, 1, g_par)])
-    foreign.sort(key=lambda k: (not first(k), not topo.may_write(cores[k], core), k))
-    for k in foreign:
-        d = combine(k, [("res%d" % k, ways(L["server"][ch, k], [core]))])
+    wait("v", d_zs)
+    combine(rank, gated(0, o_own, T.b6, g_own, T.rs[:, 256 * rank:256 * rank + 256]), True)
+    combine(p, gated(1, o_par, T.b7, g_par, T.rs[:, 256 * p:256 * p + 256]))
+    for k in sorted(foreign, key=lambda k: (slow(k), not first(k), k)):
+        d = combine(k, ("res%d" % k, ways(L["server"][ch, k], [core])))
     wait("d", d)
     g.sync.dma_start(T.y[:, :], T.ys[:, 0:NT]).then_inc(T.sem.dy, 16)
     g.sync.wait_ge(T.sem.dy, 16)

@@ -4,28 +4,28 @@ from concourse.mybir import AluOpType as A, ActivationFunctionType as F
 N, NT, CP = 8, 4096, 256
 NX = NT + CP
 ZC = NX // 16
-X1 = 2048
+XC = [0, 1536, 2816, NT]
 
 SCRATCH = {
     "pk": ("sbuf", [128, 8], "int32"), "rk": ("sbuf", [128, 8], "int32"), "tk": ("sbuf", [128, 8], "int32"),
-    "t1": ("sbuf", [128, 8], "int32"), "ds": ("sbuf", [128, 8], "float32"), "dd": ("sbuf", [128, 8], "float32"),
+    "t12": ("sbuf", [128, 16], "int32"), "dss": ("sbuf", [128, 24], "float32"),
     "ror": ("sbuf", [128, 64], "bfloat16"), "rp": ("sbuf", [128, 64], "float32"), "scn": ("sbuf", [128, 64], "float32"),
     "a32": ("sbuf", [128, 8], "int32"), "v32": ("sbuf", [128, 8], "int32"), "ibits": ("sbuf", [128, 32], "int32"),
     "ff": ("sbuf", [128, 40], "float32"),
     "nb": ("sbuf", [128, 1024], "bfloat16"), "oh": ("sbuf", [128, 1024], "bfloat16"), "ol": ("sbuf", [128, 1024], "bfloat16"),
-    "tabs": ("sbuf", [128, 1024], "uint16"),
+    "tabo": ("sbuf", [128, 128], "uint16"), "tabs": ("sbuf", [128, 256], "uint16"),
     "ones": ("sbuf", [128, 128], "bfloat16"), "tri": ("sbuf", [128, 128], "bfloat16"),
     "iob": ("sbuf", [128, 128], "bfloat16"), "ion": ("sbuf", [128, 128], "bfloat16"),
     "padc": ("sbuf", [128, 128], "bfloat16"), "c4k": ("sbuf", [128, 128], "bfloat16"), "u256": ("sbuf", [128, 64], "bfloat16"),
     "upat": ("sbuf", [128, 64], "float32"), "seg": ("sbuf", [128, 64], "float32"),
-    "ip": ("sbuf", [128, 4], "int32"), "ic": ("sbuf", [128, 4], "int32"), "ih": ("sbuf", [128, 4], "int32"),
-    "e8i": ("sbuf", [128, 4], "int32"), "e8": ("sbuf", [128, 4], "uint16"),
+    "ii": ("sbuf", [128, 16], "int32"), "e8": ("sbuf", [128, 4], "uint16"),
     "onesf": ("sbuf", [128, 256], "float32"), "diag": ("sbuf", [128, 256], "float32"),
     "iobf": ("sbuf", [128, 128], "float32"), "iorc": ("sbuf", [128, 256], "float32"),
     "expi": ("sbuf", [128, 16], "int32"), "expu": ("sbuf", [128, 16], "uint16"),
-    "spay": ("sbuf", [128, 24], "float32"), "rlp": ("sbuf", [128, 24], "float32"),
-    "gob": ("sbuf", [128, 256], "float32"), "goc": ("sbuf", [128, 256], "float32"), "gor": ("sbuf", [128, 256], "float32"),
-    "gws": ("sbuf", [128, 32], "float32"), "gx": ("sbuf", [128, 512], "float32"), "gbs": ("sbuf", [128, 512], "float32"),
+    "spay": ("sbuf", [128, 24], "float32"), "lpay": ("sbuf", [128, 24], "float32"), "rlp": ("sbuf", [128, 24], "float32"),
+    "gob": ("sbuf", [128, 512], "float32"), "goc": ("sbuf", [128, 512], "float32"), "gor": ("sbuf", [128, 512], "float32"),
+    "gws": ("sbuf", [128, 64], "float32"), "gx": ("sbuf", [128, 1024], "float32"), "gbs": ("sbuf", [128, 1024], "float32"),
+    "gin": ("sbuf", [128, 512], "float32"),
     "wo": ("sbuf", [128, 512], "float32"), "sw": ("sbuf", [128, 512], "float32"), "rlw": ("sbuf", [128, 512], "float32"),
     "xs": ("sbuf", [128, NX], "float32"), "ys": ("sbuf", [128, NX], "float32"),
     "vt": ("sbuf", [128, 2048], "float32"), "tv": ("sbuf", [128, 512], "float32"),
@@ -33,8 +33,8 @@ SCRATCH = {
 }
 for _i in range(8):
     SCRATCH["b%d" % _i] = ("psum", [128, 512], "float32")
-SEMAPHORES = (["cg", "cv", "cs", "ct", "loc", "wsent", "dpick", "dgate", "dw0", "dw1", "dx", "dy", "pay", "rpay", "w0", "w1",
-               "rw0", "rw1", "tok0", "tok1"]
+SEMAPHORES = (["cg", "cv", "cs", "ct", "loc", "sent", "dpick", "dgate", "dw0", "dw1", "dx", "dy", "pay", "lpay", "rpay",
+               "w0", "w1", "rw0", "rw1", "fw0", "fw1", "tok0", "tok1", "gat0", "gat1"]
               + ["tab%d" % k for k in range(N)] + ["res%d" % k for k in range(N)])
 
 
@@ -45,20 +45,42 @@ def layout(T, topo):
     for c in cores:
         if topo.chip(c) not in chips:
             chips.append(topo.chip(c))
+    home = [topo.chip(c) for c in cores]
 
     def free(c):
         return all(topo.may_write(c, d) for d in cores if d != c)
 
-    members = {ch: [k for k in range(N) if topo.chip(cores[k]) == ch] for ch in chips}
-    partner = {k: [q for q in members[topo.chip(cores[k])] if q != k][0] for k in range(N)}
+    members = {ch: [k for k in range(N) if home[k] == ch] for ch in chips}
+    partner = {k: [q for q in members[home[k]] if q != k][0] for k in range(N)}
+    pos = [2 * chips.index(home[k]) + members[home[k]].index(k) for k in range(N)]
     helpers = {ch: [c for c in every if topo.chip(c) == ch and c not in cores] for ch in chips}
-    relays = {}
+    relays, taken = {}, set()
     for k in range(N):
-        ports = [h for h in helpers[topo.chip(cores[k])] if free(h)]
+        ports = [h for h in helpers[home[k]] if free(h) and h not in taken]
         near = [h for h in ports if topo.die(h) == topo.die(cores[k])]
         far = [h for h in ports if topo.die(h) != topo.die(cores[k])]
-        use = (near or far) if free(cores[k]) else (far or near)
-        relays[k] = [use[0], use[-1]]
+        first = ((near or far) if free(cores[k]) else (far or near))[0]
+        left = [h for h in helpers[home[k]] if h not in taken and h != first]
+        left.sort(key=lambda h: (topo.die(h) != topo.die(first), free(h)))
+        relays[k] = [first, left[0]]
+        taken.update(relays[k])
+    gater, gates, trelay = {}, {}, {}
+    for ch in chips:
+        spare = [h for h in helpers[ch] if h not in taken]
+        for k, h in zip(members[ch], spare):
+            gater[k] = h
+            gates[h] = k
+        for k in members[ch]:
+            for c in chips:
+                if c != ch and not topo.may_write(cores[k], cores[members[c][0]]):
+                    trelay[c, k] = [h for h in spare if free(h)][0]
+    wrelay = {}
+    for ch in chips:
+        m = [c for c in range(topo.CHIPS) if topo.mates(c, ch)][0]
+        ports = [c for c in every if topo.chip(c) == m and topo.may_write(c, cores[members[ch][0]])]
+        for k in range(N):
+            if home[k] != ch and not topo.same_plane(home[k], ch):
+                wrelay[ch, k] = [c for c in ports if topo.die(c) == topo.die(relays[k][1])][0]
     server, serves = {}, {}
     for ch in chips:
         left = list(helpers[ch])
@@ -69,25 +91,24 @@ def layout(T, topo):
             left.remove(h)
             server[ch, k] = h
             serves[h] = k
-    far_servers = {k: [server[ch, k] for ch in chips if ch != topo.chip(cores[k])] for k in range(N)}
-    tab = {k: [cores[q] for q in range(N) if q not in (k, partner[k])] for k in range(N)}
+    turn = {k: [chips[(chips.index(home[k]) + i) % len(chips)] for i in range(1, len(chips))] for k in range(N)}
     order = {}
     for ch in chips:
-        for i, h in enumerate(helpers[ch]):
-            m = members[ch]
-            order[h] = m if i % 2 == 0 else m[::-1]
-    return {"cores": cores, "chips": chips, "members": members, "relays": relays, "server": server, "serves": serves,
-            "pay": far_servers, "partner": partner, "tab": tab, "order": order}
+        for relayed in (True, False):
+            for i, k in enumerate(k for k in range(N) if home[k] != ch and ((ch, k) in trelay) == relayed):
+                m = members[ch]
+                order[server[ch, k]] = m if i % 2 == 0 else m[::-1]
+    lane = {k: [c for c in chips if c == home[k] or topo.same_plane(c, home[k])].index(home[k]) for k in range(N)}
+    return {"cores": cores, "chips": chips, "home": home, "members": members, "relays": relays, "server": server,
+            "serves": serves, "partner": partner, "order": order, "pos": pos, "gater": gater, "gates": gates,
+            "wrelay": wrelay, "trelay": trelay, "turn": turn, "lane": lane}
 
 
 def rank_program(g, core, T, topo):
     L = layout(T, topo)
-    cores = L["cores"]
+    cores, home, turn, server, lane = L["cores"], L["home"], L["turn"], L["server"], L["lane"]
     ch = topo.chip(core)
-    if ch not in L["chips"]:
-        return
     rank = T.rank_of(core)
-    pair = L["members"][ch]
     Q = {"g": g, "v": g.vector, "s": g.scalar, "t": g.tensor, "d": g.sync}
     V, S, P = g.vector, g.scalar, g.tensor
     count, seen = {"loc": 0}, {}
@@ -104,24 +125,30 @@ def rank_program(g, core, T, topo):
         ins.then_inc(T.sem[name], 1)
         return (name, count[name])
 
+    def deal(m, i, n):
+        own = [b for b in range(m.bit_length()) if m >> b & 1][i::n]
+        return sum(1 << b for b in own)
+
     def engines(src, dsts, i=0, n=1):
         m = topo.mask(src, dsts[0])
         for d in dsts[1:]:
             m &= topo.mask(src, d)
-        bits = [b for b in range(m.bit_length()) if m >> b & 1][i::n]
-        return sum(1 << b for b in bits)
+        return deal(m, i, n)
 
     def inner(src, dst):
         return topo.mask(src, dst) & ~topo.mask(src, [c for c in cores if topo.chip(c) != topo.chip(src)][0])
 
+    def bits(m):
+        return bin(m).count("1")
+
     def ways(src, dsts, i=0, n=1):
-        return bin(engines(src, dsts, i, n)).count("1")
+        return bits(engines(src, dsts, i, n))
 
     def send(*transfers):
         n, out = len(transfers), []
         for i, (targets, src, rsem, *own) in enumerate(transfers):
             m = own[0] if own else engines(core, [c for c, ap in targets], i, n)
-            count["loc"] += bin(m).count("1")
+            count["loc"] += bits(m)
             ids = []
             for c, ap in targets:
                 rid, pid, se = topo.addr(c)
@@ -134,40 +161,68 @@ def rank_program(g, core, T, topo):
                                          dsts=[ap for c, ap in targets]))
         g.remote_dma_fused(out, local_sem=T.sem.loc)
 
-    def direct(k, dsts):
-        return [d for d in dsts if topo.may_write(cores[k], d)]
+    def relayed(k):
+        far = [c for c in turn[k] if (c, k) in L["trelay"]]
+        return (L["trelay"][far[0], k] if far else None), far
 
-    def passed(k, dsts):
-        far = [c for c in L["chips"] if not topo.may_write(cores[k], cores[L["members"][c][0]])]
-        out = {}
-        for d in dsts:
-            if not topo.may_write(cores[k], d):
-                out.setdefault(L["relays"][k][far.index(topo.chip(d)) % 2], []).append(d)
-        return out
+    def pay_plan(k):
+        relay, far = relayed(k)
+        direct = [server[c, k] for c in turn[k] if c not in far]
+        n = 2 if far else 1
+        m = inner(cores[k], L["gater"][k])
+        out = [(direct, engines(cores[k], direct), "pay")]
+        if far:
+            out.append(([relay], deal(m, 1, n), "rpay"))
+        return out + [([L["gater"][k]], deal(m, 0, n), "lpay")]
 
-    def arrival(k, dsts, to):
-        if topo.chip(to) == topo.chip(cores[k]):
-            return bin(inner(cores[k], to)).count("1")
-        for q, ds in passed(k, dsts).items():
-            if to in ds:
-                return ways(q, ds)
-        return ways(cores[k], direct(k, dsts))
+    def tab_plan(k):
+        relay, far = relayed(k)
+        p = cores[L["partner"][k]]
+        m = inner(cores[k], p)
+        near = [c for c in turn[k] if c not in far]
+        parts = 4
+        out = []
+        for i, c in enumerate(near):
+            d = [cores[q] for q in L["members"][c]]
+            out.append((d, engines(cores[k], d, i, parts) if len(near) > 1 else engines(cores[k], d), c))
+        for i, c in enumerate(far):
+            out.append(([relay], deal(m, i, parts), c))
+        e = m
+        for d, x, c in out:
+            e &= ~x
+        return out + [([p], e, home[k])]
 
-    def share(k, dsts, place0, sem0, place, sem, src):
-        near = [cores[L["partner"][k]]] + list(passed(k, dsts))
-        send(([(c, place0) for c in near], src, sem0, inner(core, near[0])),
-             ([(c, place) for c in direct(k, dsts)], src, sem, engines(core, direct(k, dsts))))
+    def pay_arrival(k, to):
+        relay, far = relayed(k)
+        if topo.chip(to) in far:
+            return ways(relay, [server[c, k] for c in far])
+        return [bits(m) for d, m, s in pay_plan(k) if to in d][0]
+
+    def tab_arrival(k, to):
+        relay, far = relayed(k)
+        if topo.chip(to) in far:
+            return ways(relay, [to], 0, len(far))
+        return sum(bits(m) for d, m, c in tab_plan(k) if to in d)
+
+    def chip_cols(c):
+        i = 32 * L["chips"].index(c)
+        return T.tabo[:, i:i + 32]
+
+    def tab_place(k):
+        return T.tabs[:, 32 * k:32 * k + 32]
+
+    def w2_place(k):
+        return T.rlw[:, 256 * lane[k]:256 * lane[k] + 256]
 
     def io(out, pat, base=0, cm=0):
         return done("g", g.iota(out, pat, base, cm, allow_small_or_imprecise_dtypes=True))
 
-    def gate_fills():
-        return done("v", V.memset(T.gws[:, :], 0.0)), done("v", V.memset(T.onesf[:, :], 1.0))
-
-    def gate_consts(rl, d0, d1):
+    def gate_consts(rl):
+        d0 = done("v", V.memset(T.gws[:, :], 0.0))
+        d1 = done("v", V.memset(T.onesf[:, :], 1.0))
         io(T.iobf[:, :], [[0, 8], [1, 16]])
         for i, r in enumerate(rl):
-            io(T.iorc[:, 128 * i:128 * i + 128], [[0, 8], [1, 16]], 16 * r)
+            io(T.iorc[:, 128 * i:128 * i + 128], [[0, 8], [1, 16]], 16 * L["pos"][r])
         done("g", g.iota(T.expi[:, :], [[1, 16]], 0, 0))
         wait("g", d1)
         wait("s", d0)
@@ -203,122 +258,174 @@ def rank_program(g, core, T, topo):
         wait("s", d)
         return done("s", S.activation(T.gbs[:, c:c + 256], bank[:, 0:256], F.Copy))
 
-    def expert(w, wdeps, rhs, rdeps, h0, h1, ob, i, between=None):
-        wait("t", wdeps[0], *rdeps)
-        hp, c, e = [h0, h1], [], []
-        for f in range(2):
-            c.append(done("t", P.matmul(out=hp[f][:, 0:256], lhsT=w[:, 128 * f:128 * f + 128], rhs=rhs, start=True, stop=True)))
-        for f in range(2):
+    def factors(pay, dep, i0, free=()):
+        wait("v", dep)
+        two = [i0, i0 + 1]
+        hots = [gate_hots(pay, i, i - i0) for i in two]
+        rows = [gate_table(hots[i - i0], i, T["b%d" % (i - i0)], *free) for i in two]
+        rows = [gate_row(rows[i - i0], i, T["b%d" % (i - i0)]) for i in two]
+        gx = [spread_rows(rows[i - i0], i) for i in two]
+        return [spread_all(gx[i - i0], i, T["b%d" % (i - i0)], rows[i - i0]) for i in two]
+
+    def first_layer(w, dep, rhs, rdeps, h0, h1):
+        wait("t", dep, *rdeps)
+        return [done("t", P.matmul(out=h[:, 0:256], lhsT=w[:, 128 * f:128 * f + 128], rhs=rhs, start=True, stop=True))
+                for f, h in enumerate((h0, h1))]
+
+    def rectify(q, c, h0, h1, i):
+        e = []
+        for f, h in enumerate((h0, h1)):
             a = 512 * i + 256 * f
-            wait("s", c[f])
-            e.append(done("s", S.activation(T.hs[:, a:a + 256], hp[f][:, 0:256], F.Relu)))
-        mid = between() if between else None
-        wait("t", wdeps[1])
+            wait(q, c[f])
+            if q == "v":
+                e.append(done("v", V.tensor_scalar(T.hs[:, a:a + 256], h[:, 0:256], 0.0, None, A.max)))
+            else:
+                e.append(done("s", S.activation(T.hs[:, a:a + 256], h[:, 0:256], F.Relu)))
+        return e
+
+    def second_layer(w, dep, e, ob, i, lo=0, hi=256):
+        wait("t", dep)
         for f in range(2):
             a = 512 * i + 256 * f
             wait("t", e[f])
-            ins = P.matmul(out=ob[:, 0:256], lhsT=w[:, 256 + 128 * f:384 + 128 * f], rhs=T.hs[:, a:a + 256], start=f == 0, stop=f == 1)
-        return done("t", ins), mid
-
-    def gated(i, o, bank, gd, out):
-        wait("v", o, gd)
-        return done("v", V.tensor_tensor(out, bank[:, 0:256], T.gbs[:, 256 * i:256 * i + 256], A.mult))
+            ins = P.matmul(out=ob[:, lo:hi], lhsT=w[:, 256 + 128 * f:384 + 128 * f], rhs=T.hs[:, a + lo:a + hi], start=f == 0, stop=f == 1)
+        return done("t", ins)
 
     def finish():
         for name in ("cg", "cv", "cs", "ct", "loc"):
             if count.get(name, 0):
                 wait("g", (name, count[name]))
 
+    if ch not in L["chips"]:
+        target = [c for c in L["chips"] if topo.mates(c, ch)]
+        if not target:
+            return
+        dst = target[0]
+        for k in range(N):
+            if L["wrelay"].get((dst, k)) == core:
+                wait("g", ("fw%d" % lane[k], ways(L["relays"][k][1], [core])))
+                send(([(server[dst, k], T.sw[:, 256:512])], w2_place(k), "w1"))
+        finish()
+        return
+
+    pair = L["members"][ch]
+
     if rank is None:
         k = L["serves"][core]
-        wait("v", gate_consts(pair, *gate_fills()))
-        d = done("v", V.tensor_copy(T.expu[:, :], T.expi[:, :]))
-        for f in range(2):
-            for q in pair:
-                if L["relays"][q][f] == core:
-                    wait("g", ("rw%d" % f, ways(cores[q], [core], f, 2)))
-                    send(([(h, T.sw[:, 256 * f:256 * f + 256]) for h in L["pay"][q]], T.rlw[:, 256 * f:256 * f + 256], "w%d" % f))
+        wait("v", gate_consts(pair))
+        wait("v", done("v", V.tensor_copy(T.expu[:, :], T.expi[:, :])))
+
+        def to_partner(q, f):
+            c = cores[L["partner"][q]]
+            send(([(c, T.sw[:, 256 * f:256 * f + 256])], T.rlw[:, 256 * f:256 * f + 256], "w%d" % f, inner(core, c)))
+
         for q in pair:
-            if core in passed(q, L["pay"][q]):
-                wait("g", ("rpay", arrival(q, L["pay"][q], core)))
-                send(([(c, T.spay[:, :]) for c in passed(q, L["pay"][q])[core]], T.rlp[:, :], "pay"))
-                col = T.tabs[:, 128 * q:128 * q + 128]
-                wait("g", ("tab%d" % q, arrival(q, L["tab"][q], core)))
-                send(([(c, col) for c in passed(q, L["tab"][q])[core]], col, "tab%d" % q))
-        wait("v", d, ("pay", arrival(k, L["pay"][k], core)))
-        hots = [gate_hots(T.spay, i, i) for i in range(2)]
-        rows = [gate_table(hots[i], i, T["b%d" % i]) for i in range(2)]
-        rows = [gate_row(rows[i], i, T["b%d" % i]) for i in range(2)]
-        gd = [spread_all(spread_rows(rows[i], i), i, T["b%d" % i], rows[i]) for i in range(2)]
-        wd = [("w%d" % f, ways(L["relays"][k][f], L["pay"][k])) for f in range(2)]
+            if L["relays"][q][0] == core:
+                wait("g", ("rw0", ways(cores[q], [core], 0, 2)))
+                send(([(server[c, q], T.sw[:, 0:256]) for c in turn[q]], T.rlw[:, 0:256], "w0"))
+                to_partner(q, 0)
+            if L["relays"][q][1] == core:
+                wait("g", ("rw1", ways(cores[q], [core], 1, 2)))
+                far = [L["wrelay"][c, q] for c in turn[q] if (c, q) in L["wrelay"]]
+                near = [server[c, q] for c in turn[q] if (c, q) not in L["wrelay"]]
+                send(([(h, w2_place(q)) for h in far], T.rlw[:, 256:512], "fw%d" % lane[q]))
+                send(([(h, T.sw[:, 256:512]) for h in near], T.rlw[:, 256:512], "w1"))
+                to_partner(q, 1)
+        for q in pair:
+            relay, far = relayed(q)
+            if relay == core:
+                wait("g", ("rpay", pay_arrival(q, core)))
+                send(([(server[c, q], T.spay[:, :]) for c in far], T.rlp[:, :], "pay"))
+                wait("g", ("tab%d" % q, tab_arrival(q, core)))
+                send(*[([(cores[r], tab_place(q)) for r in L["members"][c]], tab_place(i), "tab%d" % q) for i, c in enumerate(far)])
+        free = ()
+        if core in L["gates"]:
+            q = L["gates"][core]
+            free = factors(T.lpay, ("lpay", pay_arrival(q, core)), 2)
+            wait("g", *free)
+            send(*[([(cores[r], T.gin[:, 256 * (r != q):256 * (r != q) + 256])], T.gbs[:, 512 + 256 * i:768 + 256 * i],
+                    "gat%d" % (r != q)) for i, r in enumerate(pair)])
+        gd = factors(T.spay, ("pay", pay_arrival(k, core)), 0, free)
+        wd = [("w0", ways(L["relays"][k][0], [server[c, k] for c in turn[k]])),
+              ("w1", ways(L["wrelay"].get((ch, k), L["relays"][k][1]), [core]))]
         for r in L["order"][core]:
             i = pair.index(r)
-            ob, res = T["b%d" % (6 + i)], T.rs[:, 256 * i:256 * i + 256]
-            d, _ = expert(T.sw, wd, T.tv[:, 256 * i:256 * i + 256], [("tok%d" % i, ways(cores[r], [core], 0, 2))],
-                          T["b%d" % (2 + 2 * i)], T["b%d" % (3 + 2 * i)], ob, i)
-            wait("g", gated(i, d, ob, gd[i], res))
+            h0, h1, ob = T["b%d" % (2 + 2 * i)], T["b%d" % (3 + 2 * i)], T["b%d" % (6 + i)]
+            res = T.rs[:, 256 * i:256 * i + 256]
+            c = first_layer(T.sw, wd[0], T.tv[:, 256 * i:256 * i + 256], [("tok%d" % i, ways(cores[r], [core], 0, 2))], h0, h1)
+            d = second_layer(T.sw, wd[1], rectify("s", c, h0, h1, i), ob, i)
+            wait("v", d, gd[i])
+            wait("g", done("v", V.tensor_tensor(res, ob[:, 0:256], T.gbs[:, 256 * i:256 * i + 256], A.mult)))
             send(([(cores[r], T.rs[:, 256 * k:256 * k + 256])], res, "res%d" % k))
         finish()
         return
 
     p = L["partner"][rank]
     me = pair.index(rank)
+    first = lambda k: L["order"][server[ch, k]][0] == rank
+    slow = lambda k: (ch, k) in L["trelay"]
     foreign = [k for k in range(N) if k not in pair]
-    first = lambda k: L["order"][L["server"][ch, k]][0] == rank
-    slow = lambda k: not topo.may_write(cores[k], core)
-    foreign.sort(key=lambda k: (slow(k), not first(k), k))
+    foreign.sort(key=lambda k: (not first(k), slow(k), k))
+    gather_order = foreign[0:2] + [foreign[3], foreign[2]] + foreign[4:6]
 
     g.sync.dma_start(T.pk[:, :], T.pick[:, :]).then_inc(T.sem.dpick, 16)
     g.sync.dma_start(T.ff[:, 0:8], T.gate[:, :]).then_inc(T.sem.dgate, 16)
     S.dma_start(T.wo[:, 0:256], T.w1[:, :]).then_inc(T.sem.dw0, 16)
     S.dma_start(T.wo[:, 256:512], T.w2[:, :]).then_inc(T.sem.dw1, 16)
-    g.sync.dma_start(T.xs[:, 0:X1], T.x[:, 0:X1]).then_inc(T.sem.dx, 16)
-    g.sync.wait_ge(T.sem.wsent, 1)
-    g.sync.dma_start(T.xs[:, X1:NT], T.x[:, X1:NT]).then_inc(T.sem.dx, 16)
+    g.sync.dma_start(T.xs[:, 0:XC[1]], T.x[:, 0:XC[1]]).then_inc(T.sem.dx, 16)
+    for i in (1, 2):
+        g.sync.wait_ge(T.sem.sent, i)
+        g.sync.dma_start(T.xs[:, XC[i]:XC[i + 1]], T.x[:, XC[i]:XC[i + 1]]).then_inc(T.sem.dx, 16)
 
-    done("g", g.iota(T.ip[:, :], [[0, 4]], 0, 1))
-    d_e8 = done("g", g.iota(T.ic[:, :], [[2, 4]], 0, 0))
+    half = N // 2
+    assert all(L["pos"][r] == 2 * (r % half) + r // half for r in range(N))
+    done("g", g.iota(T.ii[:, 0:4], [[0, 4]], 0, 1))
+    d_e8 = done("g", g.iota(T.ii[:, 4:8], [[2, 4]], 0, 0))
     d_up = io(T.upat[:, :], [[0, 8], [1, 8]])
-    io(T.u256[0:1, :], [[0, 8], [256, 8]])
+    io(T.u256[0:1, :], [[0, 8], [256, 2], [512, 4]])
     d_one = done("v", V.memset(T.ones[:, :], 1.0))
     d_zs = done("v", V.memset(T.ys[:, 0:ZC], 0.0))
     done("v", V.memset(T.c4k[0:1, :], float(NT)))
     wait("v", d_e8)
-    d = done("v", V.tensor_scalar(T.ih[:, :], T.ip[:, :], 3, 1, A.arith_shift_right, A.bitwise_and))
+    d = done("v", V.tensor_scalar(T.ii[:, 8:12], T.ii[:, 0:4], 3, 1, A.arith_shift_right, A.bitwise_and))
     wait("v", d)
-    d = done("v", V.tensor_tensor(T.e8i[:, :], T.ih[:, :], T.ic[:, :], A.add))
+    d = done("v", V.tensor_tensor(T.ii[:, 12:16], T.ii[:, 8:12], T.ii[:, 4:8], A.add))
     wait("v", d, d_up)
-    done("v", V.tensor_copy(T.e8[:, :], T.e8i[:, :]))
+    done("v", V.tensor_copy(T.e8[:, :], T.ii[:, 12:16]))
     d_seg = done("v", V.tensor_scalar(T.seg[:, :], T.upat[:, :], 0.0, None, A.is_gt))
-    fills = gate_fills()
+    d_pad = done("v", V.memset(T.xs[:, NT:NX], 0.0))
     wait("g", d_one)
     done("g", g.affine_select(T.tri[:, :], T.ones[:, :], [[1, 128]], A.is_gt, 0.0, 0, -1))
-    io(T.iob[:, :], [[0, 8], [1, 16]])
-    io(T.ion[:, :], [[1, 128]])
-    d_cst = io(T.padc[0:1, :], [[0, 8], [16, 16]])
+    d_tri = io(T.iob[:, :], [[0, 8], [1, 16]])
     for i in range(4):
         wait("s", d_zs)
         d_zs = done("s", S.activation(T.ys[:, ZC << i:ZC << i + 1], T.ys[:, 0:ZC << i], F.Copy))
 
     wait("g", ("dw0", 16), ("dw1", 16))
     send(*[([(L["relays"][rank][f], T.rlw[:, 256 * f:256 * f + 256])], T.wo[:, 256 * f:256 * f + 256], "rw%d" % f) for f in range(2)])
-    g.sem_inc(T.sem.wsent, 1)
+    g.sem_inc(T.sem.sent, 1)
+    io(T.ion[:, :], [[1, 128]])
+    d_cst = io(T.padc[0:1, :], [[0, 8], [16, 16]])
 
     wait("v", ("dpick", 16))
     d = done("v", V.tensor_scalar(T.rk[:, :], T.pk[:, :], 12, None, A.arith_shift_right))
+    done("v", V.tensor_scalar(T.tk[:, :], T.pk[:, :], 4095, None, A.bitwise_and))
     wait("v", d, d_seg)
     d_r = done("v", V.tensor_tensor(T.ror[:, :], T.rk[:, :].indirect(T.e8[:, :]), T.upat[:, :], A.is_equal))
-    done("v", V.tensor_scalar(T.tk[:, :], T.pk[:, :], 4095, None, A.bitwise_and))
-    d = done("v", V.tensor_scalar(T.t1[:, :], T.pk[:, :], 4, 1792, A.arith_shift_right, A.bitwise_and))
+    d = done("v", V.tensor_scalar(T.t12[:, 0:8], T.pk[:, :], 3, 1536, A.arith_shift_right, A.bitwise_and))
+    d_2 = done("v", V.tensor_scalar(T.t12[:, 8:16], T.pk[:, :], 6, 256, A.arith_shift_right, A.bitwise_and))
     wait("v", d)
-    d = done("v", V.tensor_tensor(T.ds[:, :], T.tk[:, :], T.t1[:, :], A.add))
+    d = done("v", V.tensor_tensor(T.dss[:, 0:8], T.tk[:, :], T.t12[:, 0:8], A.add))
+    wait("v", d, d_2)
+    d = done("v", V.tensor_tensor(T.dss[:, 8:16], T.dss[:, 0:8], T.t12[:, 8:16], A.add))
     wait("v", d)
-    done("v", V.tensor_scalar(T.dd[:, :], T.ds[:, :], -1.0, float(NT), A.mult, A.add))
-    wait("t", d_r, d_cst)
+    done("v", V.tensor_scalar(T.dss[:, 16:24], T.dss[:, 8:16], -1.0, float(NT), A.mult, A.add))
+    wait("t", d_r, d_tri)
     P.matmul(out=T.b0[:, 0:64], lhsT=T.tri[:, :], rhs=T.ror[:, 0:64], start=True, stop=False)
     for s in range(1, 8):
         P.matmul(out=T.b0[:, 8 * s:64], lhsT=T.ones[:, :], rhs=T.ror[:, 0:64 - 8 * s], start=False, stop=False)
     d = done("t", P.matmul(out=T.b0[:, 0:64], lhsT=T.ones[0:1, :], rhs=T.u256[0:1, :], start=False, stop=True))
+    wait("t", d_cst)
     P.matmul(out=T.b1[:, 0:128], lhsT=T.ones[0:1, :], rhs=T.c4k[0:1, :], start=True, stop=False)
     P.matmul(out=T.b1[:, 0:128], lhsT=T.ones[0:1, :], rhs=T.padc[0:1, :], start=False, stop=False)
     P.matmul(out=T.b1[:, 0:128], lhsT=T.iob[0:1, :], rhs=T.ones[0:1, :], start=False, stop=False)
@@ -328,7 +435,7 @@ def rank_program(g, core, T, topo):
     d = done("v", V.tensor_tensor_scan(T.scn[:, :], T.seg[:, :], T.rp[:, :], 0.0, A.mult, A.add))
     wait("v", d)
     d_a = done("v", V.tensor_copy(T.a32[:, :], T.scn[:, 7:64:8]))
-    d_v = done("v", V.tensor_tensor(T.v32[:, :], T.scn[:, 7:64:8], T.dd[:, :], A.add))
+    d_v = done("v", V.tensor_tensor(T.v32[:, :], T.scn[:, 7:64:8], T.dss[:, 16:24], A.add))
     wait("v", d_a)
     done("v", V.tensor_scalar(T.ibits[:, 0:8], T.a32[:, :], 15, None, A.bitwise_and))
     d_a = done("v", V.tensor_scalar(T.ibits[:, 8:16], T.a32[:, :], 4, None, A.arith_shift_right))
@@ -352,72 +459,66 @@ def rank_program(g, core, T, topo):
         ins = P.matmul(out=T.b1[:, 0:128], lhsT=T.nb[:, a:b], rhs=T.ol[:, a:b], start=False, stop=m == 7)
     d = done("t", ins)
     wait("v", d)
-    d_tab = done("v", V.tensor_copy(T.tabs[:, 128 * rank:128 * rank + 128], T.b1[:, 0:128]))
+    d_tab = done("v", V.tensor_copy(T.tabo[:, :], T.b1[:, 0:128]))
 
-    col = T.tabs[:, 128 * rank:128 * rank + 128]
     wait("g", d_ff, ("dgate", 16))
-    share(rank, L["pay"][rank], T.rlp[:, :], "rpay", T.spay[:, :], "pay", T.ff[:, 0:24])
-    d_gc = gate_consts([rank], *fills)
+    places = {"lpay": T.lpay, "pay": T.spay, "rpay": T.rlp}
+    send(*[([(c, places[s][:, :]) for c in d], T.ff[:, 0:24], s, m) for d, m, s in pay_plan(rank)])
+    g.sem_inc(T.sem.sent, 1)
     wait("g", d_tab)
-    share(rank, L["tab"][rank], col, "tab%d" % rank, col, "tab%d" % rank, col)
-    send(([(cores[p], T.sw[:, :])], T.wo[:, :], "w0"))
-
-    d_pad = done("v", V.memset(T.xs[:, NT:NX], 0.0))
-    wait("v", d_gc)
-    d = done("v", V.tensor_copy(T.expu[:, :], T.expi[:, :]))
-    wait("v", d, ("dgate", 16))
-    h_own = gate_hots(T.ff, 0, 0)
-    wait("v", ("rpay", arrival(p, L["pay"][p], core)))
-    h_par = gate_hots(T.rlp, 1, 0)
+    relay, far = relayed(rank)
+    send(*[([(c, tab_place(far.index(x)) if c == relay else tab_place(rank)) for c in d], chip_cols(x), "tab%d" % rank, m)
+           for d, m, x in tab_plan(rank)])
 
     def table(k):
-        return d_tab if k == rank else ("tab%d" % k, arrival(k, L["tab"][k], core))
+        return d_tab if k == rank else ("tab%d" % k, tab_arrival(k, core))
+
+    def offsets(k, lo=0, hi=16):
+        i = 16 * L["pos"][rank] if k == rank else 32 * k + 16 * me
+        return (T.tabo if k == rank else T.tabs)[:, i + lo:i + hi]
 
     def gather(q, k):
-        wait(q, ("dx", 32), d_pad, table(k))
-        c = 128 * k + 16 * rank
-        out, src = T.vt[:, 256 * k:256 * k + 256], T.xs[:, :].indirect(T.tabs[:, c:c + 16])
+        wait(q, ("dx", 48), d_pad, table(k))
+        out, src = T.vt[:, 256 * k:256 * k + 256], T.xs[:, :].indirect(offsets(k))
         if q == "v":
             return done("v", V.tensor_copy(out, src))
         return done("s", S.activation(out, src, F.Copy))
 
-    def deliver(ks, *deps):
-        wait("g", *deps)
-        send(*[([(L["server"][ch, k], T.tv[:, 256 * me:256 * me + 256])], T.vt[:, 256 * k:256 * k + 256], "tok%d" % me) for k in ks])
+    for i in range(0, 6, 2):
+        ks = gather_order[i:i + 2]
+        wait("g", *[gather("s", k) for k in ks])
+        send(*[([(server[ch, k], T.tv[:, 256 * me:256 * me + 256])], T.vt[:, 256 * k:256 * k + 256], "tok%d" % me) for k in ks])
 
-    v_own = gather("s", rank)
-    o_own, _ = expert(T.wo, [("dw0", 16), ("dw1", 16)], T.vt[:, 256 * rank:256 * rank + 256], [v_own], T.b2, T.b3, T.b6, 0)
-    deliver(foreign[0:2], gather("s", foreign[0]), gather("v", foreign[1]))
-    deliver(foreign[2:4], gather("s", foreign[2]), gather("v", foreign[3]))
-    v_par = gather("s", p)
-    t_own, t_par = gate_table(h_own, 0, T.b0, d_tab), gate_table(h_par, 1, T.b1, d_tab)
-    r_own = gate_row(t_own, 0, T.b0)
-    m_own = spread_rows(r_own, 0)
-    r_par = gate_row(t_par, 1, T.b1)
-    g_own = spread_all(m_own, 0, T.b0, r_own)
-    deliver(foreign[4:6], gather("v", foreign[4]), gather("v", foreign[5]))
-    m_par = spread_rows(r_par, 1)
-    pw = ("w0", ways(cores[p], [core]))
-    o_par, g_par = expert(T.sw, [pw, pw], T.vt[:, 256 * p:256 * p + 256], [v_par], T.b4, T.b5, T.b7, 1,
-                          lambda: spread_all(m_par, 1, T.b1, r_par))
-
-    def combine(k, dep, start=False):
+    def combine(k, dep, start=False, lo=0, hi=256):
         wait("v", dep)
-        win, res = T.ys[:, :], T.rs[:, 256 * k:256 * k + 256]
-        c = 128 * k + 16 * rank
-        off = T.tabs[:, c:c + 16]
+        win, res = T.ys[:, :], T.rs[:, 256 * k + lo:256 * k + hi]
+        off = offsets(k, lo // 16, hi // 16)
         if not start:
             wait("v", ("cv", count["cv"]), table(k))
-            done("v", V.tensor_tensor(T.tmp[:, :], win.indirect(off), res, A.add))
-            res = T.tmp[:, :]
+            done("v", V.tensor_tensor(T.tmp[:, lo:hi], win.indirect(off), res, A.add))
+            res = T.tmp[:, lo:hi]
         wait("v", ("cv", count["cv"]))
         return done("v", V.tensor_copy(win.indirect(off), res))
 
+    def gated(i, k, o, ob, lo=0, hi=256):
+        wait("v", o, ("gat%d" % i, ways(L["gater"][k], [core], me, 2)))
+        return done("v", V.tensor_tensor(T.rs[:, 256 * k + lo:256 * k + hi], ob[:, lo:hi], T.gin[:, 256 * i + lo:256 * i + hi], A.mult))
+
+    pw = [("w%d" % f, bits(inner(L["relays"][p][f], core))) for f in range(2)]
+    v_own, v_par = gather("v", rank), gather("v", p)
+    c_own = first_layer(T.wo, ("dw0", 16), T.vt[:, 256 * rank:256 * rank + 256], [v_own], T.b2, T.b3)
+    e_own = rectify("v", c_own, T.b2, T.b3, 0)
+    o_own = second_layer(T.wo, ("dw1", 16), e_own, T.b6, 0)
+    c_par = first_layer(T.sw, pw[0], T.vt[:, 256 * p:256 * p + 256], [v_par], T.b4, T.b5)
     wait("v", d_zs)
-    combine(rank, gated(0, o_own, T.b6, g_own, T.rs[:, 256 * rank:256 * rank + 256]), True)
-    combine(p, gated(1, o_par, T.b7, g_par, T.rs[:, 256 * p:256 * p + 256]))
-    for k in sorted(foreign, key=lambda k: (slow(k), not first(k), k)):
-        d = combine(k, ("res%d" % k, ways(L["server"][ch, k], [core])))
+    combine(rank, gated(0, rank, o_own, T.b6), True)
+    e_par = rectify("v", c_par, T.b4, T.b5, 1)
+    parts = [(T.b7, 0, 128), (T.b0, 128, 256)]
+    o_par = [second_layer(T.sw, pw[1], e_par, ob, 1, lo, hi) for ob, lo, hi in parts]
+    for o, (ob, lo, hi) in zip(o_par, parts):
+        combine(p, gated(1, p, o, ob, lo, hi), False, lo, hi)
+    for k in foreign:
+        d = combine(k, ("res%d" % k, ways(server[ch, k], [core])))
     wait("d", d)
     g.sync.dma_start(T.y[:, :], T.ys[:, 0:NT]).then_inc(T.sem.dy, 16)
     g.sync.wait_ge(T.sem.dy, 16)

from concourse.bass import DstId, RemoteDMATransfer
from concourse.mybir import AluOpType as A, ActivationFunctionType as F

N, NT, CP = 8, 4096, 256
NX = NT + CP
ZC = NX // 16
XC = [0, 1536, 2816, NT]

SCRATCH = {
    "pk": ("sbuf", [128, 8], "int32"), "rk": ("sbuf", [128, 8], "int32"), "tk": ("sbuf", [128, 8], "int32"),
    "t12": ("sbuf", [128, 16], "int32"), "dss": ("sbuf", [128, 24], "float32"),
    "ror": ("sbuf", [128, 64], "bfloat16"), "rp": ("sbuf", [128, 64], "float32"), "scn": ("sbuf", [128, 64], "float32"),
    "a32": ("sbuf", [128, 8], "int32"), "v32": ("sbuf", [128, 8], "int32"), "ibits": ("sbuf", [128, 32], "int32"),
    "ff": ("sbuf", [128, 40], "float32"),
    "nb": ("sbuf", [128, 1024], "bfloat16"), "oh": ("sbuf", [128, 1024], "bfloat16"), "ol": ("sbuf", [128, 1024], "bfloat16"),
    "tabo": ("sbuf", [128, 128], "uint16"), "tabs": ("sbuf", [128, 256], "uint16"),
    "ones": ("sbuf", [128, 128], "bfloat16"), "tri": ("sbuf", [128, 128], "bfloat16"),
    "iob": ("sbuf", [128, 128], "bfloat16"), "ion": ("sbuf", [128, 128], "bfloat16"),
    "padc": ("sbuf", [128, 128], "bfloat16"), "c4k": ("sbuf", [128, 128], "bfloat16"), "u256": ("sbuf", [128, 64], "bfloat16"),
    "upat": ("sbuf", [128, 64], "float32"), "seg": ("sbuf", [128, 64], "float32"),
    "ii": ("sbuf", [128, 16], "int32"), "e8": ("sbuf", [128, 4], "uint16"),
    "onesf": ("sbuf", [128, 256], "float32"), "diag": ("sbuf", [128, 256], "float32"),
    "iobf": ("sbuf", [128, 128], "float32"), "iorc": ("sbuf", [128, 256], "float32"),
    "expi": ("sbuf", [128, 16], "int32"), "expu": ("sbuf", [128, 16], "uint16"),
    "spay": ("sbuf", [128, 24], "float32"), "lpay": ("sbuf", [128, 24], "float32"), "rlp": ("sbuf", [128, 24], "float32"),
    "gob": ("sbuf", [128, 512], "float32"), "goc": ("sbuf", [128, 512], "float32"), "gor": ("sbuf", [128, 512], "float32"),
    "gws": ("sbuf", [128, 64], "float32"), "gx": ("sbuf", [128, 1024], "float32"), "gbs": ("sbuf", [128, 1024], "float32"),
    "gin": ("sbuf", [128, 512], "float32"),
    "wo": ("sbuf", [128, 512], "float32"), "sw": ("sbuf", [128, 512], "float32"), "rlw": ("sbuf", [128, 512], "float32"),
    "xs": ("sbuf", [128, NX], "float32"), "ys": ("sbuf", [128, NX], "float32"),
    "vt": ("sbuf", [128, 2048], "float32"), "tv": ("sbuf", [128, 512], "float32"),
    "hs": ("sbuf", [128, 1024], "float32"), "rs": ("sbuf", [128, 2048], "float32"), "tmp": ("sbuf", [128, 256], "float32"),
}
for _i in range(8):
    SCRATCH["b%d" % _i] = ("psum", [128, 512], "float32")
SEMAPHORES = (["cg", "cv", "cs", "ct", "loc", "sent", "dpick", "dgate", "dw0", "dw1", "dx", "dy", "pay", "lpay", "rpay",
               "w0", "w1", "rw0", "rw1", "fw0", "fw1", "tok0", "tok1", "gat0", "gat1"]
              + ["tab%d" % k for k in range(N)] + ["res%d" % k for k in range(N)])


def layout(T, topo):
    cores = list(T.cores)
    every = range(topo.CHIPS * topo.CORES_PER_CHIP)
    chips = []
    for c in cores:
        if topo.chip(c) not in chips:
            chips.append(topo.chip(c))
    home = [topo.chip(c) for c in cores]

    def free(c):
        return all(topo.may_write(c, d) for d in cores if d != c)

    members = {ch: [k for k in range(N) if home[k] == ch] for ch in chips}
    partner = {k: [q for q in members[home[k]] if q != k][0] for k in range(N)}
    pos = [2 * chips.index(home[k]) + members[home[k]].index(k) for k in range(N)]
    helpers = {ch: [c for c in every if topo.chip(c) == ch and c not in cores] for ch in chips}
    relays, taken = {}, set()
    for k in range(N):
        ports = [h for h in helpers[home[k]] if free(h) and h not in taken]
        near = [h for h in ports if topo.die(h) == topo.die(cores[k])]
        far = [h for h in ports if topo.die(h) != topo.die(cores[k])]
        first = ((near or far) if free(cores[k]) else (far or near))[0]
        left = [h for h in helpers[home[k]] if h not in taken and h != first]
        left.sort(key=lambda h: (topo.die(h) != topo.die(first), free(h)))
        relays[k] = [first, left[0]]
        taken.update(relays[k])
    gater, gates, trelay = {}, {}, {}
    for ch in chips:
        spare = [h for h in helpers[ch] if h not in taken]
        for k, h in zip(members[ch], spare):
            gater[k] = h
            gates[h] = k
        for k in members[ch]:
            for c in chips:
                if c != ch and not topo.may_write(cores[k], cores[members[c][0]]):
                    trelay[c, k] = [h for h in spare if free(h)][0]
    wrelay = {}
    for ch in chips:
        m = [c for c in range(topo.CHIPS) if topo.mates(c, ch)][0]
        ports = [c for c in every if topo.chip(c) == m and topo.may_write(c, cores[members[ch][0]])]
        for k in range(N):
            if home[k] != ch and not topo.same_plane(home[k], ch):
                wrelay[ch, k] = [c for c in ports if topo.die(c) == topo.die(relays[k][1])][0]
    server, serves = {}, {}
    for ch in chips:
        left = list(helpers[ch])
        foreign = [k for k in range(N) if k not in members[ch]]
        for k in sorted(foreign, key=lambda q: (not free(cores[q]), q)):
            die = topo.die(relays[k][0])
            h = ([c for c in left if topo.die(c) == die] or left)[0]
            left.remove(h)
            server[ch, k] = h
            serves[h] = k
    turn = {k: [chips[(chips.index(home[k]) + i) % len(chips)] for i in range(1, len(chips))] for k in range(N)}
    order = {}
    for ch in chips:
        for relayed in (True, False):
            for i, k in enumerate(k for k in range(N) if home[k] != ch and ((ch, k) in trelay) == relayed):
                m = members[ch]
                order[server[ch, k]] = m if i % 2 == 0 else m[::-1]
    lane = {k: [c for c in chips if c == home[k] or topo.same_plane(c, home[k])].index(home[k]) for k in range(N)}
    return {"cores": cores, "chips": chips, "home": home, "members": members, "relays": relays, "server": server,
            "serves": serves, "partner": partner, "order": order, "pos": pos, "gater": gater, "gates": gates,
            "wrelay": wrelay, "trelay": trelay, "turn": turn, "lane": lane}


def rank_program(g, core, T, topo):
    L = layout(T, topo)
    cores, home, turn, server, lane = L["cores"], L["home"], L["turn"], L["server"], L["lane"]
    ch = topo.chip(core)
    rank = T.rank_of(core)
    Q = {"g": g, "v": g.vector, "s": g.scalar, "t": g.tensor, "d": g.sync}
    V, S, P = g.vector, g.scalar, g.tensor
    count, seen = {"loc": 0}, {}

    def wait(q, *deps):
        for sem, val in deps:
            if seen.get((q, sem), 0) < val:
                Q[q].wait_ge(T.sem[sem], val)
                seen[q, sem] = val

    def done(q, ins):
        name = "c" + q
        count[name] = count.get(name, 0) + 1
        ins.then_inc(T.sem[name], 1)
        return (name, count[name])

    def deal(m, i, n):
        own = [b for b in range(m.bit_length()) if m >> b & 1][i::n]
        return sum(1 << b for b in own)

    def engines(src, dsts, i=0, n=1):
        m = topo.mask(src, dsts[0])
        for d in dsts[1:]:
            m &= topo.mask(src, d)
        return deal(m, i, n)

    def inner(src, dst):
        return topo.mask(src, dst) & ~topo.mask(src, [c for c in cores if topo.chip(c) != topo.chip(src)][0])

    def bits(m):
        return bin(m).count("1")

    def ways(src, dsts, i=0, n=1):
        return bits(engines(src, dsts, i, n))

    def send(*transfers):
        n, out = len(transfers), []
        for i, (targets, src, rsem, *own) in enumerate(transfers):
            m = own[0] if own else engines(core, [c for c, ap in targets], i, n)
            count["loc"] += bits(m)
            ids = []
            for c, ap in targets:
                rid, pid, se = topo.addr(c)
                ids.append(DstId(rid=rid, pnc=pid))
            if n == 1 and len(targets) == 1:
                g.remote_dma(out_ap=targets[0][1], in_ap=src, remote_sem=T.sem[rsem], local_sem=T.sem.loc, pid=pid,
                             routing_id=rid, dma_engine_mask=m)
                return
            out.append(RemoteDMATransfer(dst_ids=ids, dma_engine_mask=m, remote_sem=T.sem[rsem], srcs=[src],
                                         dsts=[ap for c, ap in targets]))
        g.remote_dma_fused(out, local_sem=T.sem.loc)

    def relayed(k):
        far = [c for c in turn[k] if (c, k) in L["trelay"]]
        return (L["trelay"][far[0], k] if far else None), far

    def pay_plan(k):
        relay, far = relayed(k)
        direct = [server[c, k] for c in turn[k] if c not in far]
        n = 2 if far else 1
        m = inner(cores[k], L["gater"][k])
        out = [(direct, engines(cores[k], direct), "pay")]
        if far:
            out.append(([relay], deal(m, 1, n), "rpay"))
        return out + [([L["gater"][k]], deal(m, 0, n), "lpay")]

    def tab_plan(k):
        relay, far = relayed(k)
        p = cores[L["partner"][k]]
        m = inner(cores[k], p)
        near = [c for c in turn[k] if c not in far]
        parts = 4
        out = []
        for i, c in enumerate(near):
            d = [cores[q] for q in L["members"][c]]
            out.append((d, engines(cores[k], d, i, parts) if len(near) > 1 else engines(cores[k], d), c))
        for i, c in enumerate(far):
            out.append(([relay], deal(m, i, parts), c))
        e = m
        for d, x, c in out:
            e &= ~x
        return out + [([p], e, home[k])]

    def pay_arrival(k, to):
        relay, far = relayed(k)
        if topo.chip(to) in far:
            return ways(relay, [server[c, k] for c in far])
        return [bits(m) for d, m, s in pay_plan(k) if to in d][0]

    def tab_arrival(k, to):
        relay, far = relayed(k)
        if topo.chip(to) in far:
            return ways(relay, [to], 0, len(far))
        return sum(bits(m) for d, m, c in tab_plan(k) if to in d)

    def chip_cols(c):
        i = 32 * L["chips"].index(c)
        return T.tabo[:, i:i + 32]

    def tab_place(k):
        return T.tabs[:, 32 * k:32 * k + 32]

    def w2_place(k):
        return T.rlw[:, 256 * lane[k]:256 * lane[k] + 256]

    def io(out, pat, base=0, cm=0):
        return done("g", g.iota(out, pat, base, cm, allow_small_or_imprecise_dtypes=True))

    def gate_consts(rl):
        d0 = done("v", V.memset(T.gws[:, :], 0.0))
        d1 = done("v", V.memset(T.onesf[:, :], 1.0))
        io(T.iobf[:, :], [[0, 8], [1, 16]])
        for i, r in enumerate(rl):
            io(T.iorc[:, 128 * i:128 * i + 128], [[0, 8], [1, 16]], 16 * L["pos"][r])
        done("g", g.iota(T.expi[:, :], [[1, 16]], 0, 0))
        wait("g", d1)
        wait("s", d0)
        return done("g", g.affine_select(T.diag[:, :], T.onesf[:, :], [[0, 16], [1, 16]], A.is_equal, 0.0, 0, -1))

    def gate_hots(pay, i, c):
        a, b = 128 * i, 128 * i + 128
        d = done("v", V.tensor_tensor(T.goc[:, a:b], pay[:, 16:24].indirect(T.expu[:, 0:8]), T.iorc[:, 128 * c:128 * c + 128], A.is_equal))
        done("v", V.tensor_tensor(T.gob[:, a:b], pay[:, 8:16].indirect(T.expu[:, 0:8]), T.iobf[:, :], A.is_equal))
        wait("v", d)
        return done("v", V.tensor_tensor(T.gor[:, a:b], pay[:, 0:8].indirect(T.expu[:, 0:8]), T.goc[:, a:b], A.mult))

    def gate_table(d, i, bank, *free):
        wait("t", d, *free)
        for m in range(8):
            a = 128 * i + 16 * m
            ins = P.matmul(out=bank[0:16, 0:16], lhsT=T.gob[:, a:a + 16], rhs=T.gor[:, a:a + 16], start=m == 0, stop=m == 7)
        return done("t", ins)

    def gate_row(d, i, bank):
        wait("s", d)
        return done("s", S.activation(T.gws[0:16, 16 * i:16 * i + 16], bank[0:16, 0:16], F.Copy))

    def spread_rows(d, i):
        wait("v", d)
        c = 256 * i
        return done("v", V.tensor_tensor(T.gx[:, c:c + 256], T.gws[:, 16 * i:16 * i + 16].indirect(T.expu[:, :]), T.diag[:, :], A.mult))

    def spread_all(d, i, bank, *free):
        c = 256 * i
        wait("t", d, *free)
        d = done("t", P.matmul(out=bank[:, 0:256], lhsT=T.onesf[0:16, 0:128], rhs=T.gx[0:16, c:c + 256], start=True, stop=True))
        wait("s", d)
        return done("s", S.activation(T.gbs[:, c:c + 256], bank[:, 0:256], F.Copy))

    def factors(pay, dep, i0, free=()):
        wait("v", dep)
        two = [i0, i0 + 1]
        hots = [gate_hots(pay, i, i - i0) for i in two]
        rows = [gate_table(hots[i - i0], i, T["b%d" % (i - i0)], *free) for i in two]
        rows = [gate_row(rows[i - i0], i, T["b%d" % (i - i0)]) for i in two]
        gx = [spread_rows(rows[i - i0], i) for i in two]
        return [spread_all(gx[i - i0], i, T["b%d" % (i - i0)], rows[i - i0]) for i in two]

    def first_layer(w, dep, rhs, rdeps, h0, h1):
        wait("t", dep, *rdeps)
        return [done("t", P.matmul(out=h[:, 0:256], lhsT=w[:, 128 * f:128 * f + 128], rhs=rhs, start=True, stop=True))
                for f, h in enumerate((h0, h1))]

    def rectify(q, c, h0, h1, i):
        e = []
        for f, h in enumerate((h0, h1)):
            a = 512 * i + 256 * f
            wait(q, c[f])
            if q == "v":
                e.append(done("v", V.tensor_scalar(T.hs[:, a:a + 256], h[:, 0:256], 0.0, None, A.max)))
            else:
                e.append(done("s", S.activation(T.hs[:, a:a + 256], h[:, 0:256], F.Relu)))
        return e

    def second_layer(w, dep, e, ob, i, lo=0, hi=256):
        wait("t", dep)
        for f in range(2):
            a = 512 * i + 256 * f
            wait("t", e[f])
            ins = P.matmul(out=ob[:, lo:hi], lhsT=w[:, 256 + 128 * f:384 + 128 * f], rhs=T.hs[:, a + lo:a + hi], start=f == 0, stop=f == 1)
        return done("t", ins)

    def finish():
        for name in ("cg", "cv", "cs", "ct", "loc"):
            if count.get(name, 0):
                wait("g", (name, count[name]))

    if ch not in L["chips"]:
        target = [c for c in L["chips"] if topo.mates(c, ch)]
        if not target:
            return
        dst = target[0]
        for k in range(N):
            if L["wrelay"].get((dst, k)) == core:
                wait("g", ("fw%d" % lane[k], ways(L["relays"][k][1], [core])))
                send(([(server[dst, k], T.sw[:, 256:512])], w2_place(k), "w1"))
        finish()
        return

    pair = L["members"][ch]

    if rank is None:
        k = L["serves"][core]
        wait("v", gate_consts(pair))
        wait("v", done("v", V.tensor_copy(T.expu[:, :], T.expi[:, :])))

        def to_partner(q, f):
            c = cores[L["partner"][q]]
            send(([(c, T.sw[:, 256 * f:256 * f + 256])], T.rlw[:, 256 * f:256 * f + 256], "w%d" % f, inner(core, c)))

        for q in pair:
            if L["relays"][q][0] == core:
                wait("g", ("rw0", ways(cores[q], [core], 0, 2)))
                send(([(server[c, q], T.sw[:, 0:256]) for c in turn[q]], T.rlw[:, 0:256], "w0"))
                to_partner(q, 0)
            if L["relays"][q][1] == core:
                wait("g", ("rw1", ways(cores[q], [core], 1, 2)))
                far = [L["wrelay"][c, q] for c in turn[q] if (c, q) in L["wrelay"]]
                near = [server[c, q] for c in turn[q] if (c, q) not in L["wrelay"]]
                send(([(h, w2_place(q)) for h in far], T.rlw[:, 256:512], "fw%d" % lane[q]))
                send(([(h, T.sw[:, 256:512]) for h in near], T.rlw[:, 256:512], "w1"))
                to_partner(q, 1)
        for q in pair:
            relay, far = relayed(q)
            if relay == core:
                wait("g", ("rpay", pay_arrival(q, core)))
                send(([(server[c, q], T.spay[:, :]) for c in far], T.rlp[:, :], "pay"))
                wait("g", ("tab%d" % q, tab_arrival(q, core)))
                send(*[([(cores[r], tab_place(q)) for r in L["members"][c]], tab_place(i), "tab%d" % q) for i, c in enumerate(far)])
        free = ()
        if core in L["gates"]:
            q = L["gates"][core]
            free = factors(T.lpay, ("lpay", pay_arrival(q, core)), 2)
            wait("g", *free)
            send(*[([(cores[r], T.gin[:, 256 * (r != q):256 * (r != q) + 256])], T.gbs[:, 512 + 256 * i:768 + 256 * i],
                    "gat%d" % (r != q)) for i, r in enumerate(pair)])
        gd = factors(T.spay, ("pay", pay_arrival(k, core)), 0, free)
        wd = [("w0", ways(L["relays"][k][0], [server[c, k] for c in turn[k]])),
              ("w1", ways(L["wrelay"].get((ch, k), L["relays"][k][1]), [core]))]
        for r in L["order"][core]:
            i = pair.index(r)
            h0, h1, ob = T["b%d" % (2 + 2 * i)], T["b%d" % (3 + 2 * i)], T["b%d" % (6 + i)]
            res = T.rs[:, 256 * i:256 * i + 256]
            c = first_layer(T.sw, wd[0], T.tv[:, 256 * i:256 * i + 256], [("tok%d" % i, ways(cores[r], [core], 0, 2))], h0, h1)
            d = second_layer(T.sw, wd[1], rectify("s", c, h0, h1, i), ob, i)
            wait("v", d, gd[i])
            wait("g", done("v", V.tensor_tensor(res, ob[:, 0:256], T.gbs[:, 256 * i:256 * i + 256], A.mult)))
            send(([(cores[r], T.rs[:, 256 * k:256 * k + 256])], res, "res%d" % k))
        finish()
        return

    p = L["partner"][rank]
    me = pair.index(rank)
    first = lambda k: L["order"][server[ch, k]][0] == rank
    slow = lambda k: (ch, k) in L["trelay"]
    foreign = [k for k in range(N) if k not in pair]
    foreign.sort(key=lambda k: (not first(k), slow(k), k))
    gather_order = foreign[0:2] + [foreign[3], foreign[2]] + foreign[4:6]

    g.sync.dma_start(T.pk[:, :], T.pick[:, :]).then_inc(T.sem.dpick, 16)
    g.sync.dma_start(T.ff[:, 0:8], T.gate[:, :]).then_inc(T.sem.dgate, 16)
    S.dma_start(T.wo[:, 0:256], T.w1[:, :]).then_inc(T.sem.dw0, 16)
    S.dma_start(T.wo[:, 256:512], T.w2[:, :]).then_inc(T.sem.dw1, 16)
    g.sync.dma_start(T.xs[:, 0:XC[1]], T.x[:, 0:XC[1]]).then_inc(T.sem.dx, 16)
    for i in (1, 2):
        g.sync.wait_ge(T.sem.sent, i)
        g.sync.dma_start(T.xs[:, XC[i]:XC[i + 1]], T.x[:, XC[i]:XC[i + 1]]).then_inc(T.sem.dx, 16)

    half = N // 2
    assert all(L["pos"][r] == 2 * (r % half) + r // half for r in range(N))
    done("g", g.iota(T.ii[:, 0:4], [[0, 4]], 0, 1))
    d_e8 = done("g", g.iota(T.ii[:, 4:8], [[2, 4]], 0, 0))
    d_up = io(T.upat[:, :], [[0, 8], [1, 8]])
    io(T.u256[0:1, :], [[0, 8], [256, 2], [512, 4]])
    d_one = done("v", V.memset(T.ones[:, :], 1.0))
    d_zs = done("v", V.memset(T.ys[:, 0:ZC], 0.0))
    done("v", V.memset(T.c4k[0:1, :], float(NT)))
    wait("v", d_e8)
    d = done("v", V.tensor_scalar(T.ii[:, 8:12], T.ii[:, 0:4], 3, 1, A.arith_shift_right, A.bitwise_and))
    wait("v", d)
    d = done("v", V.tensor_tensor(T.ii[:, 12:16], T.ii[:, 8:12], T.ii[:, 4:8], A.add))
    wait("v", d, d_up)
    done("v", V.tensor_copy(T.e8[:, :], T.ii[:, 12:16]))
    d_seg = done("v", V.tensor_scalar(T.seg[:, :], T.upat[:, :], 0.0, None, A.is_gt))
    d_pad = done("v", V.memset(T.xs[:, NT:NX], 0.0))
    wait("g", d_one)
    done("g", g.affine_select(T.tri[:, :], T.ones[:, :], [[1, 128]], A.is_gt, 0.0, 0, -1))
    d_tri = io(T.iob[:, :], [[0, 8], [1, 16]])
    for i in range(4):
        wait("s", d_zs)
        d_zs = done("s", S.activation(T.ys[:, ZC << i:ZC << i + 1], T.ys[:, 0:ZC << i], F.Copy))

    wait("g", ("dw0", 16), ("dw1", 16))
    send(*[([(L["relays"][rank][f], T.rlw[:, 256 * f:256 * f + 256])], T.wo[:, 256 * f:256 * f + 256], "rw%d" % f) for f in range(2)])
    g.sem_inc(T.sem.sent, 1)
    io(T.ion[:, :], [[1, 128]])
    d_cst = io(T.padc[0:1, :], [[0, 8], [16, 16]])

    wait("v", ("dpick", 16))
    d = done("v", V.tensor_scalar(T.rk[:, :], T.pk[:, :], 12, None, A.arith_shift_right))
    done("v", V.tensor_scalar(T.tk[:, :], T.pk[:, :], 4095, None, A.bitwise_and))
    wait("v", d, d_seg)
    d_r = done("v", V.tensor_tensor(T.ror[:, :], T.rk[:, :].indirect(T.e8[:, :]), T.upat[:, :], A.is_equal))
    d = done("v", V.tensor_scalar(T.t12[:, 0:8], T.pk[:, :], 3, 1536, A.arith_shift_right, A.bitwise_and))
    d_2 = done("v", V.tensor_scalar(T.t12[:, 8:16], T.pk[:, :], 6, 256, A.arith_shift_right, A.bitwise_and))
    wait("v", d)
    d = done("v", V.tensor_tensor(T.dss[:, 0:8], T.tk[:, :], T.t12[:, 0:8], A.add))
    wait("v", d, d_2)
    d = done("v", V.tensor_tensor(T.dss[:, 8:16], T.dss[:, 0:8], T.t12[:, 8:16], A.add))
    wait("v", d)
    done("v", V.tensor_scalar(T.dss[:, 16:24], T.dss[:, 8:16], -1.0, float(NT), A.mult, A.add))
    wait("t", d_r, d_tri)
    P.matmul(out=T.b0[:, 0:64], lhsT=T.tri[:, :], rhs=T.ror[:, 0:64], start=True, stop=False)
    for s in range(1, 8):
        P.matmul(out=T.b0[:, 8 * s:64], lhsT=T.ones[:, :], rhs=T.ror[:, 0:64 - 8 * s], start=False, stop=False)
    d = done("t", P.matmul(out=T.b0[:, 0:64], lhsT=T.ones[0:1, :], rhs=T.u256[0:1, :], start=False, stop=True))
    wait("t", d_cst)
    P.matmul(out=T.b1[:, 0:128], lhsT=T.ones[0:1, :], rhs=T.c4k[0:1, :], start=True, stop=False)
    P.matmul(out=T.b1[:, 0:128], lhsT=T.ones[0:1, :], rhs=T.padc[0:1, :], start=False, stop=False)
    P.matmul(out=T.b1[:, 0:128], lhsT=T.iob[0:1, :], rhs=T.ones[0:1, :], start=False, stop=False)
    wait("v", d)
    d = done("v", V.tensor_tensor(T.rp[:, :], T.b0[:, 0:64], T.ror[:, :], A.mult))
    wait("v", d)
    d = done("v", V.tensor_tensor_scan(T.scn[:, :], T.seg[:, :], T.rp[:, :], 0.0, A.mult, A.add))
    wait("v", d)
    d_a = done("v", V.tensor_copy(T.a32[:, :], T.scn[:, 7:64:8]))
    d_v = done("v", V.tensor_tensor(T.v32[:, :], T.scn[:, 7:64:8], T.dss[:, 16:24], A.add))
    wait("v", d_a)
    done("v", V.tensor_scalar(T.ibits[:, 0:8], T.a32[:, :], 15, None, A.bitwise_and))
    d_a = done("v", V.tensor_scalar(T.ibits[:, 8:16], T.a32[:, :], 4, None, A.arith_shift_right))
    wait("v", d_v)
    done("v", V.tensor_scalar(T.ibits[:, 16:24], T.v32[:, :], 8128, None, A.bitwise_and))
    d_v = done("v", V.tensor_scalar(T.ibits[:, 24:32], T.v32[:, :], 63, None, A.bitwise_and))
    wait("v", d_a)
    d_ff = done("v", V.tensor_copy(T.ff[:, 8:24], T.ibits[:, 0:16]))
    wait("v", d_v)
    d_fv = done("v", V.tensor_copy(T.ff[:, 24:40], T.ibits[:, 16:32]))
    wait("v", d_ff, d_cst)
    for m in range(8):
        done("v", V.tensor_scalar(T.nb[:, 128 * m:128 * m + 128], T.iob[:, :], T.ff[:, 8 + m:9 + m], -1.0, A.is_equal, A.mult))
    wait("v", d_fv)
    for m in range(8):
        a, b = 128 * m, 128 * m + 128
        done("v", V.tensor_scalar(T.oh[:, a:b], T.ion[:, :], T.ff[:, 16 + m:17 + m], T.ff[:, 24 + m:25 + m], A.is_equal, A.mult))
        d = done("v", V.tensor_scalar(T.ol[:, a:b], T.ion[:, :], T.ff[:, 16 + m:17 + m], T.ff[:, 32 + m:33 + m], A.is_equal, A.mult))
        wait("t", d)
        P.matmul(out=T.b1[:, 0:128], lhsT=T.nb[:, a:b], rhs=T.oh[:, a:b], start=False, stop=False)
        ins = P.matmul(out=T.b1[:, 0:128], lhsT=T.nb[:, a:b], rhs=T.ol[:, a:b], start=False, stop=m == 7)
    d = done("t", ins)
    wait("v", d)
    d_tab = done("v", V.tensor_copy(T.tabo[:, :], T.b1[:, 0:128]))

    wait("g", d_ff, ("dgate", 16))
    places = {"lpay": T.lpay, "pay": T.spay, "rpay": T.rlp}
    send(*[([(c, places[s][:, :]) for c in d], T.ff[:, 0:24], s, m) for d, m, s in pay_plan(rank)])
    g.sem_inc(T.sem.sent, 1)
    wait("g", d_tab)
    relay, far = relayed(rank)
    send(*[([(c, tab_place(far.index(x)) if c == relay else tab_place(rank)) for c in d], chip_cols(x), "tab%d" % rank, m)
           for d, m, x in tab_plan(rank)])

    def table(k):
        return d_tab if k == rank else ("tab%d" % k, tab_arrival(k, core))

    def offsets(k, lo=0, hi=16):
        i = 16 * L["pos"][rank] if k == rank else 32 * k + 16 * me
        return (T.tabo if k == rank else T.tabs)[:, i + lo:i + hi]

    def gather(q, k):
        wait(q, ("dx", 48), d_pad, table(k))
        out, src = T.vt[:, 256 * k:256 * k + 256], T.xs[:, :].indirect(offsets(k))
        if q == "v":
            return done("v", V.tensor_copy(out, src))
        return done("s", S.activation(out, src, F.Copy))

    for i in range(0, 6, 2):
        ks = gather_order[i:i + 2]
        wait("g", *[gather("s", k) for k in ks])
        send(*[([(server[ch, k], T.tv[:, 256 * me:256 * me + 256])], T.vt[:, 256 * k:256 * k + 256], "tok%d" % me) for k in ks])

    def combine(k, dep, start=False, lo=0, hi=256):
        wait("v", dep)
        win, res = T.ys[:, :], T.rs[:, 256 * k + lo:256 * k + hi]
        off = offsets(k, lo // 16, hi // 16)
        if not start:
            wait("v", ("cv", count["cv"]), table(k))
            done("v", V.tensor_tensor(T.tmp[:, lo:hi], win.indirect(off), res, A.add))
            res = T.tmp[:, lo:hi]
        wait("v", ("cv", count["cv"]))
        return done("v", V.tensor_copy(win.indirect(off), res))

    def gated(i, k, o, ob, lo=0, hi=256):
        wait("v", o, ("gat%d" % i, ways(L["gater"][k], [core], me, 2)))
        return done("v", V.tensor_tensor(T.rs[:, 256 * k + lo:256 * k + hi], ob[:, lo:hi], T.gin[:, 256 * i + lo:256 * i + hi], A.mult))

    pw = [("w%d" % f, bits(inner(L["relays"][p][f], core))) for f in range(2)]
    v_own, v_par = gather("v", rank), gather("v", p)
    c_own = first_layer(T.wo, ("dw0", 16), T.vt[:, 256 * rank:256 * rank + 256], [v_own], T.b2, T.b3)
    e_own = rectify("v", c_own, T.b2, T.b3, 0)
    o_own = second_layer(T.wo, ("dw1", 16), e_own, T.b6, 0)
    c_par = first_layer(T.sw, pw[0], T.vt[:, 256 * p:256 * p + 256], [v_par], T.b4, T.b5)
    wait("v", d_zs)
    combine(rank, gated(0, rank, o_own, T.b6), True)
    e_par = rectify("v", c_par, T.b4, T.b5, 1)
    parts = [(T.b7, 0, 128), (T.b0, 128, 256)]
    o_par = [second_layer(T.sw, pw[1], e_par, ob, 1, lo, hi) for ob, lo, hi in parts]
    for o, (ob, lo, hi) in zip(o_par, parts):
        combine(p, gated(1, p, o, ob, lo, hi), False, lo, hi)
    for k in foreign:
        d = combine(k, ("res%d" % k, ways(server[ch, k], [core])))
    wait("d", d)
    g.sync.dma_start(T.y[:, :], T.ys[:, 0:NT]).then_inc(T.sem.dy, 16)
    g.sync.wait_ge(T.sem.dy, 16)
    finish()
